import numpy as np
import ml_dtypes


def mxq(x, axis, fmt="e4m3"):
    dtype, down = {"e4m3": (ml_dtypes.float8_e4m3fn, 7), "e5m2": (ml_dtypes.float8_e5m2, 14)}[fmt]
    v = np.moveaxis(np.asarray(x, np.float32).astype(ml_dtypes.bfloat16).astype(np.float64), axis, -1)
    blocks = v.reshape(v.shape[:-1] + (-1, 32))
    amax = np.abs(blocks).max(-1, keepdims=True)
    byte = np.maximum(np.where(amax > 0, np.frexp(amax)[1] - 1 + 127, 0) - down, 1)
    scale = np.exp2(byte - 127.0)
    codes = (blocks / scale).astype(np.float32).astype(dtype).astype(np.float64)
    return np.moveaxis((codes * scale).reshape(v.shape), -1, axis)


WIDE = False


def mx_kscale(k):
    if not WIDE:
        return np.ones(k)
    levels = np.array([10, -10, 5, -5, 0])
    if k % 512:
        return np.exp2(np.random.permutation(np.resize(levels, k // 32))).repeat(32)
    a = np.empty((k // 512, 16))
    for p in range(k // 512):
        a[p, :8] = np.random.permutation(np.resize(levels, 8))
        for g in range(8):
            far = levels[np.abs(levels - a[p, g]) >= 10]
            a[p, g + 8] = far[np.random.randint(len(far))]
    return np.exp2(a.ravel()).repeat(32)


def f64(x):
    return np.asarray(x).astype(np.float64)


def striped(idx):
    return np.tile(idx.reshape(-1, 16).T, (8, 1)).astype(np.uint16)


def unstriped(offs):
    return offs[:16].T.reshape(-1).astype(np.int64)


def pack_weight(w):
    k, n = w.shape
    w = f64(np.asarray(w, np.float32).astype(ml_dtypes.bfloat16)).reshape(k // 32, 32, n)
    amax = np.abs(w).max(1)
    byte = np.clip(np.where(amax > 0, np.frexp(amax)[1] - 1 + 127 - 7, 1), 1, 254)
    scaled = (w * np.exp2(127.0 - byte)[:, None, :]).reshape(k, n).astype(np.float32)
    words = np.ascontiguousarray(scaled.reshape(k // 512, 128, 4, n).transpose(0, 1, 3, 2)).astype(ml_dtypes.float8_e4m3fn).view(np.uint8)
    return words, np.ascontiguousarray(byte.astype(np.uint8).reshape(k // 512, 16, n))


def unpack_weight(words, scales):
    g, p, n, _ = words.shape
    vals = np.ascontiguousarray(words).view(ml_dtypes.float8_e4m3fn).astype(np.float64) * np.repeat(np.exp2(scales.astype(np.float64) - 127.0), 8, axis=1)[..., None]
    return vals.transpose(0, 1, 3, 2).reshape(g * 512, n)


def relu(v):
    return np.maximum(v, 0.0)


K, T, S, H, R, G, W = 512, 1024, 512, 512, 512, 256, 512
P = 2 ** 7


def setup_inputs():
    n = np.random.standard_normal
    s = mx_kscale(K)[:, None]
    u = mx_kscale(H)
    packed_xT = pack_weight(n((K, T)) * s)
    return {
        "x_words": packed_xT[0],
        "x_scales": packed_xT[1],
        "w1": (n((K, H)) / np.sqrt(K) / s * u).astype(np.float32),
        "kn1": (n((H, G)) / np.sqrt(H) / u[:, None]).astype(np.float32),
        "frac1": (np.tile(np.random.uniform(0.0, 1.0, R), (P, 1))).astype(np.float32),
        "kn2": (n((H, W)) / np.sqrt(H) / u[:, None]).astype(np.float32),
        "frac2": (np.tile(np.random.uniform(0.0, 1.0, R), (P, 1))).astype(np.float32),
        "offs": striped(np.random.permutation(T)[:S]),
        "left1": striped(np.random.permutation(np.concatenate([np.arange(G), np.random.randint(0, G, R - G)]))),
        "right1": striped(np.random.permutation(np.concatenate([np.arange(G), np.random.randint(0, G, R - G)]))),
        "left2": striped(np.random.randint(0, W, R)),
        "right2": striped(np.random.randint(0, W, R)),
    }


def reference(x_words, x_scales, w1, kn1, frac1, kn2, frac2, offs, left1, right1, left2, right2):
    xq = unpack_weight(x_words, x_scales)[:, unstriped(offs)]
    h = relu(mxq(f64(w1), 0, "e4m3").T @ xq)
    hq = mxq(h, 0, "e4m3")
    kn1q = mxq(f64(kn1), 0, "e4m3")
    y1 = hq.T @ kn1q
    gl1 = y1[:, unstriped(left1)]
    kn2q = mxq(f64(kn2), 0, "e4m3")
    y2 = hq.T @ kn2q
    gl2 = y2[:, unstriped(left2)]
    return gl1 + f64(frac1)[:1] * (y1[:, unstriped(right1)] - gl1) + gl2 + f64(frac2)[:1] * (y2[:, unstriped(right2)] - gl2)

@@ -1,0 +1,247 @@
+from contextlib import ExitStack
+
+import concourse.mybir as mybir
+from concourse.masks import make_identity
+
+K, T, S, H, R, G, W = 512, 1024, 512, 512, 512, 256, 512
+FLOPS = 2 * K * H * S + 2 * H * S * (G + W)
+
+F32 = mybir.dt.float32
+BF16 = mybir.dt.bfloat16
+I32 = mybir.dt.int32
+U32 = mybir.dt.uint32
+U16 = mybir.dt.uint16
+U8 = mybir.dt.uint8
+FP8X4 = mybir.dt.float8_e4m3fn_x4
+ACT = mybir.ActivationFunctionType
+ALU = mybir.AluOpType
+
+P = 128
+PACK = 4
+TILES = S // P
+CHUNKS = R // P
+WINDOW = R + 16
+
+
+def tile_picked_ynhits_val_p_kernel(
+    tc, x_words, x_scales, w1, kn1, frac1, kn2, frac2, offs, left1, right1, left2, right2, out
+):
+    nc = tc.nc
+    with ExitStack() as ctx:
+        lists = ctx.enter_context(tc.tile_pool(name="lists", bufs=1))
+        sb = ctx.enter_context(tc.tile_pool(name="sb", bufs=1))
+        psum = ctx.enter_context(tc.psum_pool(name="psum", bufs=1))
+
+        def load_list(name, src):
+            held = lists.tile([P, R // 16], U16, name=name)
+            nc.sync.dma_start(held[:], src)
+            return held
+
+        def load(name, src, shape, dtype):
+            held = sb.tile(shape, dtype, name=name, align_bytes=64)
+            nc.sync.dma_start(held[:], src)
+            return held
+
+        def bank(number, shape, name):
+            return psum.tile(shape, F32, name=name, tag="bank%d" % number)
+
+        xs_table = sb.tile([P, T], U8, name="xs_table", align_bytes=64)
+        nc.vector.memset(xs_table[:].bitcast(I32), 0)
+        ident = sb.tile([P, P], F32, name="ident", align_bytes=64)
+        y1 = [sb.tile([P, WINDOW], F32, name="y1_%d" % t, align_bytes=64) for t in range(TILES)]
+        y2 = [sb.tile([P, WINDOW], F32, name="y2_%d" % t, align_bytes=64) for t in range(TILES)]
+        for t in range(TILES):
+            nc.gpsimd.memset(y1[t][:, G:], 0.0)
+            nc.gpsimd.memset(y2[t][:, W:], 0.0)
+        make_identity(nc, ident[:])
+
+        w1_rows = w1.rearrange("(p j) c -> p j c", j=PACK)
+        half = H // 2
+        w1_raw = [None, None]
+        w1_raw[0] = load("w1_raw0", w1_rows[:, :, :half], [P, PACK, half], F32)
+        for q in range(4):
+            nc.sync.dma_start(
+                xs_table[:].bitcast(I32)[32 * q : 32 * q + 4, :], x_scales[0].bitcast(I32)[4 * q : 4 * q + 4, :]
+            )
+        offs_sb = load_list("offs_sb", offs)
+        w1_raw[1] = load("w1_raw1", w1_rows[:, :, half:], [P, PACK, half], F32)
+        xw_table = load("xw_table", x_words[0].rearrange("p n j -> p (n j)").bitcast(I32), [P, T], I32)
+        kn1_raw = load("kn1_raw", kn1.rearrange("(p j) c -> p j c", j=PACK), [P, PACK, G], F32)
+        right1_sb = load_list("right1_sb", right1)
+        f1 = load("f1", frac1, [P, R], F32)
+        left1_sb = load_list("left1_sb", left1)
+        kn2_raw = load("kn2_raw", kn2.rearrange("(p j) c -> p j c", j=PACK), [P, PACK, W], F32)
+        right2_sb = load_list("right2_sb", right2)
+        f2 = load("f2", frac2, [P, R], F32)
+        left2_sb = load_list("left2_sb", left2)
+
+        def quantize(name, grouped, width):
+            codes = sb.tile([P, width], U32, name=name + "_codes", align_bytes=64)
+            scales = sb.tile([P, width], U8, name=name + "_scales", align_bytes=64)
+            nc.vector.quantize_mx(out=codes[:].bitcast(FP8X4), scales=scales[:], in_=grouped[:])
+            return codes, scales
+
+        def interleave(copy, grouped, raw, c0, c1):
+            copy(
+                grouped[:, PACK * c0 : PACK * c1].rearrange("p (c i j) -> p c j i", i=4, j=PACK),
+                raw[:, :, c0:c1].rearrange("p j (c i) -> p c j i", i=4),
+            )
+
+        w1_grouped = sb.tile([P, PACK * H], BF16, name="w1_grouped", align_bytes=64)
+        w1_view = w1_grouped[:].rearrange("p (e m j) -> p m e j", e=PACK, j=PACK)
+        xg_words = sb.tile([P, S], U32, name="xg_words", align_bytes=64)
+        xg_scales = sb.tile([P, S], U8, name="xg_scales", align_bytes=64)
+
+        def gather_words(c0, c1):
+            nc.vector.tensor_copy(
+                xg_words[:, c0:c1], xw_table[:].bitcast(U32).indirect(offs_sb[:, c0 // 16 : c1 // 16])
+            )
+
+        nc.scalar.copy(w1_view[:, : P // 2], w1_raw[0][:].rearrange("p j (m e) -> p m e j", e=PACK))
+        nc.vector.tensor_copy(xg_scales[:], xs_table[:].indirect(offs_sb[:]))
+        nc.vector.tensor_copy(w1_view[:, P // 2 :], w1_raw[1][:].rearrange("p j (m e) -> p m e j", e=PACK))
+        w1_codes, w1_scales = quantize("w1", w1_grouped, H)
+        gather_words(0, P)
+        gather_words(P, 2 * P)
+
+        def hidden(t):
+            cols = slice(t * P, (t + 1) * P)
+            acc = bank(t % 2, [P, PACK, P], "h_acc%d" % t)
+            for e in range(PACK):
+                ch = slice(e * P, (e + 1) * P)
+                nc.tensor.matmul_mx(
+                    out=acc[:, e, :],
+                    lhsT=w1_codes[:, ch].bitcast(FP8X4),
+                    lhsT_scale=w1_scales[:, ch],
+                    rhs=xg_words[:, cols].bitcast(FP8X4),
+                    rhs_scale=xg_scales[:, cols],
+                    start=True,
+                    stop=True,
+                )
+            grouped = sb.tile([P, PACK * P], BF16, name="h_grouped%d" % t, align_bytes=64)
+            nc.scalar.activation(
+                grouped[:].rearrange("p (n e) -> p n e", e=PACK), acc[:].rearrange("p e n -> p n e"), ACT.Relu
+            )
+            return quantize("h%d" % t, grouped, P)
+
+        def knots(number, h, kn, window, width, name):
+            acc = bank(number, [P, width], name)
+            nc.tensor.matmul_mx(
+                out=acc[:],
+                lhsT=h[0][:].bitcast(FP8X4),
+                lhsT_scale=h[1][:],
+                rhs=kn[0][:].bitcast(FP8X4),
+                rhs_scale=kn[1][:],
+                start=True,
+                stop=True,
+            )
+            nc.scalar.copy(window[:, :width], acc[:])
+
+        def complement(name, f):
+            a = sb.tile([P, R], F32, name=name, align_bytes=64)
+            nc.scalar.activation(a[:], f[:], ACT.Copy, bias=1.0, scale=-1.0)
+            return a
+
+        kn1_grouped = sb.tile([P, PACK * G], BF16, name="kn1_grouped", align_bytes=64)
+        interleave(nc.vector.tensor_copy, kn1_grouped, kn1_raw, 0, G)
+        kn1_q = quantize("kn1", kn1_grouped, G)
+        hq = [None] * TILES
+        hq[0] = hidden(0)
+        knots(2, hq[0], kn1_q, y1[0], G, "y1_acc0")
+        gather_words(2 * P, S)
+        hq[1] = hidden(1)
+        a1 = complement("a1", f1)
+        knots(3, hq[1], kn1_q, y1[1], G, "y1_acc1")
+
+        kn2_grouped = sb.tile([P, PACK * W], BF16, name="kn2_grouped", align_bytes=64)
+        for c0 in range(0, W, P):
+            interleave(nc.scalar.copy, kn2_grouped, kn2_raw, c0, c0 + P)
+        kn2_q = quantize("kn2", kn2_grouped, W)
+        knots(2, hq[0], kn2_q, y2[0], W, "y2_acc0")
+        hq[2] = hidden(2)
+        knots(3, hq[2], kn1_q, y1[2], G, "y1_acc2")
+        a2 = complement("a2", f2)
+        knots(2, hq[1], kn2_q, y2[1], W, "y2_acc1")
+        hq[3] = hidden(3)
+        knots(3, hq[2], kn2_q, y2[2], W, "y2_acc2")
+        knots(2, hq[3], kn1_q, y1[3], G, "y1_acc3")
+        knots(3, hq[3], kn2_q, y2[3], W, "y2_acc3")
+
+        terms = [[] for t in range(TILES)]
+
+        def product_tile(name, tag, width=R):
+            return sb.tile([P, width], F32, name=name, tag=tag, align_bytes=64)
+
+        def term(t, window, offsets, weight, product):
+            nc.vector.tensor_tensor(product, window[:].indirect(offsets[:]), weight[:], ALU.mult)
+            terms[t].append(product)
+
+        def r1(t, product=None):
+            term(t, y1[t], right1_sb, f1, product_tile("r1_%d" % t, "r1_%d" % t)[:] if product is None else product)
+
+        def l1(t, product=None):
+            term(t, y1[t], left1_sb, a1, product_tile("l1_%d" % t, "l1_%d" % t)[:] if product is None else product)
+
+        def r2(t, product=None):
+            term(t, y2[t], right2_sb, f2, product_tile("r2_%d" % t, "r2_%d" % t)[:] if product is None else product)
+
+        def l2(t, product=None):
+            term(t, y2[t], left2_sb, a2, product_tile("l2_%d" % t, "l2_%d" % t)[:] if product is None else product)
+
+        def tensor_sum(t, forward, back):
+            turned = bank(forward, [P, CHUNKS, P], "turned%d" % t)
+            parts = list(terms[t])
+            for c in range(CHUNKS):
+                for i, part in enumerate(parts):
+                    nc.tensor.matmul(
+                        turned[:, c, :],
+                        lhsT=part[:, c * P : (c + 1) * P],
+                        rhs=ident[:],
+                        start=(i == 0),
+                        stop=(i == len(parts) - 1),
+                        is_transpose=True,
+                    )
+            turned_sb = sb.tile([P, CHUNKS, P], F32, name="turned_sb%d" % t, align_bytes=64)
+            nc.scalar.copy(turned_sb[:], turned[:])
+            total = bank(back, [P, R], "total%d" % t)
+            for c in range(CHUNKS):
+                nc.tensor.transpose(total[:, c * P : (c + 1) * P], turned_sb[:, c, :], ident[:])
+            return total
+
+        def store(t, result):
+            nc.sync.dma_start(out[t * P : (t + 1) * P, :], result[:])
+
+        def finish_on_scalar(t, forward, back):
+            total = tensor_sum(t, forward, back)
+            result = sb.tile([P, R], F32, name="result%d" % t, align_bytes=64)
+            nc.scalar.copy(result[:], total[:])
+            store(t, result)
+
+        def finish_on_vector(t, total):
+            result = sb.tile([P, R], F32, name="result%d" % t, align_bytes=64)
+            nc.vector.tensor_tensor(result[:], total[:], terms[t][3], ALU.add)
+            store(t, result)
+
+        r1(0)
+        l1(0)
+        r1(1)
+        pair = product_tile("pair", "kn2_grouped", 2 * R)
+        l1(1, pair[:, :R])
+        r1(2, pair[:, R:])
+        r2(0)
+        l2(0)
+        finish_on_scalar(0, 4, 6)
+        r2(1)
+        l2(1)
+        finish_on_scalar(1, 5, 7)
+        l1(2, product_tile("l1_2", "y2_0")[:])
+        r2(2)
+        total2 = tensor_sum(2, 4, 0)
+        r1(3)
+        l1(3)
+        r2(3)
+        total3 = tensor_sum(3, 5, 1)
+        l2(2, product_tile("l2_2", "y1_3")[:])
+        l2(3)
+        finish_on_vector(2, total2)
+        finish_on_vector(3, total3)

@@ -50,10 +50,11 @@ def tile_picked_ynhits_val_p_kernel(
         ident = sb.tile([P, P], F32, name="ident", align_bytes=64)
         y1 = [sb.tile([P, WINDOW], F32, name="y1_%d" % t, align_bytes=64) for t in range(TILES)]
         y2 = [sb.tile([P, WINDOW], F32, name="y2_%d" % t, align_bytes=64) for t in range(TILES)]
+        nc.vector.memset(ident[:], 0.0)
+        make_identity(nc, ident[:], nomemset=True)
         for t in range(TILES):
-            nc.gpsimd.memset(y1[t][:, G:], 0.0)
-            nc.gpsimd.memset(y2[t][:, W:], 0.0)
-        make_identity(nc, ident[:])
+            nc.vector.memset(y1[t][:, G:], 0.0)
+            nc.vector.memset(y2[t][:, W:], 0.0)
 
         w1_rows = w1.rearrange("(p j) c -> p j c", j=PACK)
         half = H // 2
@@ -70,7 +71,8 @@ def tile_picked_ynhits_val_p_kernel(
         right1_sb = load_list("right1_sb", right1)
         f1 = load("f1", frac1, [P, R], F32)
         left1_sb = load_list("left1_sb", left1)
-        kn2_raw = load("kn2_raw", kn2.rearrange("(p j) c -> p j c", j=PACK), [P, PACK, W], F32)
+        kn2_rows = kn2.rearrange("(p j) c -> p j c", j=PACK)
+        kn2_raw = [load("kn2_raw%d" % u, kn2_rows[:, :, u * G : (u + 1) * G], [P, PACK, G], F32) for u in range(2)]
         right2_sb = load_list("right2_sb", right2)
         f2 = load("f2", frac2, [P, R], F32)
         left2_sb = load_list("left2_sb", left2)
@@ -104,9 +106,9 @@ def tile_picked_ynhits_val_p_kernel(
         gather_words(0, P)
         gather_words(P, 2 * P)
 
-        def hidden(t):
+        def hidden(number, t):
             cols = slice(t * P, (t + 1) * P)
-            acc = bank(t % 2, [P, PACK, P], "h_acc%d" % t)
+            acc = bank(number, [P, PACK, P], "h_acc%d" % t)
             for e in range(PACK):
                 ch = slice(e * P, (e + 1) * P)
                 nc.tensor.matmul_mx(
@@ -138,7 +140,7 @@ def tile_picked_ynhits_val_p_kernel(
             nc.scalar.copy(window[:, :width], acc[:])
 
         def complement(name, f):
-            a = sb.tile([P, R], F32, name=name, align_bytes=64)
+            a = sb.tile([P, R], F32, name=name, tag="kn2_raw1", align_bytes=64)
             nc.scalar.activation(a[:], f[:], ACT.Copy, bias=1.0, scale=-1.0)
             return a
 
@@ -146,26 +148,32 @@ def tile_picked_ynhits_val_p_kernel(
         interleave(nc.vector.tensor_copy, kn1_grouped, kn1_raw, 0, G)
         kn1_q = quantize("kn1", kn1_grouped, G)
         hq = [None] * TILES
-        hq[0] = hidden(0)
+        hq[0] = hidden(0, 0)
         knots(2, hq[0], kn1_q, y1[0], G, "y1_acc0")
         gather_words(2 * P, S)
-        hq[1] = hidden(1)
-        a1 = complement("a1", f1)
+        a1 = sb.tile([P, R], F32, name="a1", tag="h_grouped0", align_bytes=64)
+        nc.vector.tensor_scalar(a1[:], f1[:], -1.0, 1.0, ALU.mult, ALU.add)
+        hq[1] = hidden(1, 1)
         knots(3, hq[1], kn1_q, y1[1], G, "y1_acc1")
 
-        kn2_grouped = sb.tile([P, PACK * W], BF16, name="kn2_grouped", align_bytes=64)
-        for c0 in range(0, W, P):
-            interleave(nc.scalar.copy, kn2_grouped, kn2_raw, c0, c0 + P)
-        kn2_q = quantize("kn2", kn2_grouped, W)
-        knots(2, hq[0], kn2_q, y2[0], W, "y2_acc0")
-        hq[2] = hidden(2)
-        knots(3, hq[2], kn1_q, y1[2], G, "y1_acc2")
+        kn2_codes = sb.tile([P, W], U32, name="kn2_codes", align_bytes=64)
+        kn2_scales = sb.tile([P, W], U8, name="kn2_scales", align_bytes=64)
+        kn2_q = (kn2_codes, kn2_scales)
+        for u in range(2):
+            cols = slice(u * G, (u + 1) * G)
+            grouped = sb.tile([P, PACK * G], BF16, name="kn2_grouped%d" % u, align_bytes=64)
+            for c0 in range(0, G, P):
+                interleave(nc.scalar.copy, grouped, kn2_raw[u], c0, c0 + P)
+            nc.vector.quantize_mx(out=kn2_codes[:, cols].bitcast(FP8X4), scales=kn2_scales[:, cols], in_=grouped[:])
+            knots(u, hq[0], (kn2_codes[:, cols], kn2_scales[:, cols]), y2[0][:, cols], G, "y2_acc0_%d" % u)
         a2 = complement("a2", f2)
         knots(2, hq[1], kn2_q, y2[1], W, "y2_acc1")
-        hq[3] = hidden(3)
-        knots(3, hq[2], kn2_q, y2[2], W, "y2_acc2")
-        knots(2, hq[3], kn1_q, y1[3], G, "y1_acc3")
-        knots(3, hq[3], kn2_q, y2[3], W, "y2_acc3")
+        hq[2] = hidden(1, 2)
+        hq[3] = hidden(2, 3)
+        knots(3, hq[2], kn1_q, y1[2], G, "y1_acc2")
+        knots(0, hq[2], kn2_q, y2[2], W, "y2_acc2")
+        knots(3, hq[3], kn1_q, y1[3], G, "y1_acc3")
+        knots(2, hq[3], kn2_q, y2[3], W, "y2_acc3")
 
         terms = [[] for t in range(TILES)]
 
@@ -188,19 +196,17 @@ def tile_picked_ynhits_val_p_kernel(
         def l2(t, product=None):
             term(t, y2[t], left2_sb, a2, product_tile("l2_%d" % t, "l2_%d" % t)[:] if product is None else product)
 
+        def turn(turned, part, c, first, last):
+            nc.tensor.matmul(
+                turned, lhsT=part[:, c * P : (c + 1) * P], rhs=ident[:], start=first, stop=last, is_transpose=True
+            )
+
         def tensor_sum(t, forward, back):
             turned = bank(forward, [P, CHUNKS, P], "turned%d" % t)
             parts = list(terms[t])
             for c in range(CHUNKS):
                 for i, part in enumerate(parts):
-                    nc.tensor.matmul(
-                        turned[:, c, :],
-                        lhsT=part[:, c * P : (c + 1) * P],
-                        rhs=ident[:],
-                        start=(i == 0),
-                        stop=(i == len(parts) - 1),
-                        is_transpose=True,
-                    )
+                    turn(turned[:, c, :], part, c, i == 0, i == len(parts) - 1)
             turned_sb = sb.tile([P, CHUNKS, P], F32, name="turned_sb%d" % t, align_bytes=64)
             nc.scalar.copy(turned_sb[:], turned[:])
             total = bank(back, [P, R], "total%d" % t)
@@ -208,11 +214,25 @@ def tile_picked_ynhits_val_p_kernel(
                 nc.tensor.transpose(total[:, c * P : (c + 1) * P], turned_sb[:, c, :], ident[:])
             return total
 
+        def open_banks(t, numbers):
+            return [bank(n, [P, P], "turned%d_%d" % (t, c)) for c, n in enumerate(numbers)]
+
+        def add_latest(t, banks, first=False, last=False):
+            for c in range(CHUNKS):
+                turn(banks[c][:], terms[t][-1], c, first, last)
+
+        def turn_back(t, banks, back):
+            turned_sb = sb.tile([P, CHUNKS, P], F32, name="turned_sb%d" % t, align_bytes=64)
+            total = bank(back, [P, R], "total%d" % t)
+            for c in range(CHUNKS):
+                nc.scalar.copy(turned_sb[:, c, :], banks[c][:])
+                nc.tensor.transpose(total[:, c * P : (c + 1) * P], turned_sb[:, c, :], ident[:])
+            return total
+
         def store(t, result):
             nc.sync.dma_start(out[t * P : (t + 1) * P, :], result[:])
 
-        def finish_on_scalar(t, forward, back):
-            total = tensor_sum(t, forward, back)
+        def finish_on_scalar(t, total):
             result = sb.tile([P, R], F32, name="result%d" % t, align_bytes=64)
             nc.scalar.copy(result[:], total[:])
             store(t, result)
@@ -222,26 +242,51 @@ def tile_picked_ynhits_val_p_kernel(
             nc.vector.tensor_tensor(result[:], total[:], terms[t][3], ALU.add)
             store(t, result)
 
+        banks0 = open_banks(0, [4, 5, 6, 7])
         r1(0)
+        add_latest(0, banks0, first=True)
         l1(0)
-        r1(1)
-        pair = product_tile("pair", "kn2_grouped", 2 * R)
-        l1(1, pair[:, :R])
-        r1(2, pair[:, R:])
+        add_latest(0, banks0)
+        r1(1, product_tile("r1_1", "kn2_grouped0")[:])
+        l1(1, product_tile("l1_1", "kn2_grouped1")[:])
         r2(0)
+        add_latest(0, banks0)
         l2(0)
-        finish_on_scalar(0, 4, 6)
+        add_latest(0, banks0, last=True)
+        finish_on_scalar(0, turn_back(0, banks0, 1))
         r2(1)
         l2(1)
-        finish_on_scalar(1, 5, 7)
-        l1(2, product_tile("l1_2", "y2_0")[:])
-        r2(2)
-        total2 = tensor_sum(2, 4, 0)
-        r1(3)
-        l1(3)
-        r2(3)
-        total3 = tensor_sum(3, 5, 1)
-        l2(2, product_tile("l2_2", "y1_3")[:])
-        l2(3)
-        finish_on_vector(2, total2)
-        finish_on_vector(3, total3)
+        finish_on_scalar(1, tensor_sum(1, 0, 1))
+        banks2 = open_banks(2, [4, 5, 6, 7])
+        for i, gather in enumerate((r1, l1, r2, l2)):
+            gather(2)
+            add_latest(2, banks2, first=(i == 0), last=(i == 3))
+        finish_on_scalar(2, turn_back(2, banks2, 0))
+        banks3 = open_banks(3, [4, 5, 6, 7])
+        for i, gather in enumerate((r1, l1)):
+            gather(3)
+            add_latest(3, banks3, first=(i == 0))
+        halves = [slice(u * R // 2, (u + 1) * R // 2) for u in range(2)]
+
+        def half_term(u, offsets, weight, product):
+            nc.vector.tensor_tensor(
+                product[:, halves[u]], y2[3][:].indirect(offsets[:, u * 16 : (u + 1) * 16]), weight[:, halves[u]], ALU.mult
+            )
+
+        third = product_tile("r2_3", "r2_3")
+        last = product_tile("l2_3", "l2_3")
+        turned_sb = sb.tile([P, CHUNKS, P], F32, name="turned_sb3", align_bytes=64)
+        totals = [bank(2 + u, [P, R // 2], "total3_%d" % u) for u in range(2)]
+        for u in range(2):
+            half_term(u, right2_sb, f2, third)
+            for c in (2 * u, 2 * u + 1):
+                turn(banks3[c][:], third, c, False, True)
+            for c in (2 * u, 2 * u + 1):
+                nc.scalar.copy(turned_sb[:, c, :], banks3[c][:])
+                nc.tensor.transpose(totals[u][:, (c % 2) * P : (c % 2 + 1) * P], turned_sb[:, c, :], ident[:])
+        for u in range(2):
+            half_term(u, left2_sb, a2, last)
+        for u, cols in enumerate(halves):
+            result = sb.tile([P, R // 2], F32, name="result3_%d" % u, align_bytes=64)
+            nc.vector.tensor_tensor(result[:], totals[u][:], last[:, cols], ALU.add)
+            nc.sync.dma_start(out[3 * P :, cols], result[:])

@@ -139,14 +139,18 @@ def tile_picked_ynhits_val_p_kernel(
             )
             nc.scalar.copy(window[:, :width], acc[:])
 
-        def complement(name, f):
-            a = sb.tile([P, R], F32, name=name, tag="kn2_raw1", align_bytes=64)
-            nc.scalar.activation(a[:], f[:], ACT.Copy, bias=1.0, scale=-1.0)
-            return a
-
         kn1_grouped = sb.tile([P, PACK * G], BF16, name="kn1_grouped", align_bytes=64)
-        interleave(nc.vector.tensor_copy, kn1_grouped, kn1_raw, 0, G)
-        kn1_q = quantize("kn1", kn1_grouped, G)
+        kn1_codes = sb.tile([P, G], U32, name="kn1_codes", align_bytes=64)
+        kn1_scales = sb.tile([P, G], U8, name="kn1_scales", align_bytes=64)
+        kn1_q = (kn1_codes, kn1_scales)
+        for c0 in range(0, G, P):
+            interleave(nc.vector.tensor_copy, kn1_grouped, kn1_raw, c0, c0 + P)
+        for c0 in range(0, G, P):
+            nc.vector.quantize_mx(
+                out=kn1_codes[:, c0 : c0 + P].bitcast(FP8X4),
+                scales=kn1_scales[:, c0 : c0 + P],
+                in_=kn1_grouped[:, PACK * c0 : PACK * (c0 + P)],
+            )
         hq = [None] * TILES
         hq[0] = hidden(0, 0)
         knots(2, hq[0], kn1_q, y1[0], G, "y1_acc0")
@@ -166,14 +170,15 @@ def tile_picked_ynhits_val_p_kernel(
                 interleave(nc.scalar.copy, grouped, kn2_raw[u], c0, c0 + P)
             nc.vector.quantize_mx(out=kn2_codes[:, cols].bitcast(FP8X4), scales=kn2_scales[:, cols], in_=grouped[:])
             knots(u, hq[0], (kn2_codes[:, cols], kn2_scales[:, cols]), y2[0][:, cols], G, "y2_acc0_%d" % u)
-        a2 = complement("a2", f2)
-        knots(2, hq[1], kn2_q, y2[1], W, "y2_acc1")
+        after_casts = sb.tile([P, 2 * R + R // 2], F32, name="after_casts", tag="kn2_raw1", align_bytes=64)
+        a2 = after_casts[:, :R]
+        nc.scalar.activation(a2, f2[:], ACT.Copy, bias=1.0, scale=-1.0)
+        knots(0, hq[1], kn2_q, y2[1], W, "y2_acc1")
         hq[2] = hidden(1, 2)
-        hq[3] = hidden(2, 3)
-        knots(3, hq[2], kn1_q, y1[2], G, "y1_acc2")
+        hq[3] = hidden(0, 3)
+        knots(1, hq[2], kn1_q, y1[2], G, "y1_acc2")
         knots(0, hq[2], kn2_q, y2[2], W, "y2_acc2")
-        knots(3, hq[3], kn1_q, y1[3], G, "y1_acc3")
-        knots(2, hq[3], kn2_q, y2[3], W, "y2_acc3")
+        knots(0, hq[3], kn1_q, y1[3], G, "y1_acc3")
 
         terms = [[] for t in range(TILES)]
 
@@ -247,21 +252,40 @@ def tile_picked_ynhits_val_p_kernel(
         add_latest(0, banks0, first=True)
         l1(0)
         add_latest(0, banks0)
-        r1(1, product_tile("r1_1", "kn2_grouped0")[:])
-        l1(1, product_tile("l1_1", "kn2_grouped1")[:])
+        banks1 = [bank(2 + c, [P, P], "turned1_%d" % c) for c in range(2)]
+        r1_halves = [product_tile("r1_1", "kn2_raw0", R // 2)[:], after_casts[:, 2 * R :]]
+        for u in range(2):
+            nc.vector.tensor_tensor(
+                r1_halves[u],
+                y1[1][:].indirect(right1_sb[:, u * 16 : (u + 1) * 16]),
+                f1[:, u * R // 2 : (u + 1) * R // 2],
+                ALU.mult,
+            )
+        for c in range(2):
+            turn(banks1[c][:], r1_halves[0], c, True, False)
+        l1(1, after_casts[:, R : 2 * R])
+        for c in range(2):
+            turn(banks1[c][:], terms[1][0], c, False, False)
         r2(0)
         add_latest(0, banks0)
         l2(0)
         add_latest(0, banks0, last=True)
         finish_on_scalar(0, turn_back(0, banks0, 1))
+        knots(1, hq[3], kn2_q, y2[3], W, "y2_acc3")
+        banks1 = banks1 + [bank(2 + c, [P, P], "turned1_%d" % c) for c in range(2, 4)]
+        for c in range(2, 4):
+            turn(banks1[c][:], r1_halves[1], c - 2, True, False)
+            turn(banks1[c][:], terms[1][0], c, False, False)
         r2(1)
+        add_latest(1, banks1)
         l2(1)
-        finish_on_scalar(1, tensor_sum(1, 0, 1))
-        banks2 = open_banks(2, [4, 5, 6, 7])
+        add_latest(1, banks1, last=True)
+        finish_on_scalar(1, turn_back(1, banks1, 0))
+        banks2 = open_banks(2, [6, 7, 2, 3])
         for i, gather in enumerate((r1, l1, r2, l2)):
             gather(2)
             add_latest(2, banks2, first=(i == 0), last=(i == 3))
-        finish_on_scalar(2, turn_back(2, banks2, 0))
+        finish_on_scalar(2, turn_back(2, banks2, 1))
         banks3 = open_banks(3, [4, 5, 6, 7])
         for i, gather in enumerate((r1, l1)):
             gather(3)
@@ -276,7 +300,7 @@ def tile_picked_ynhits_val_p_kernel(
         third = product_tile("r2_3", "r2_3")
         last = product_tile("l2_3", "l2_3")
         turned_sb = sb.tile([P, CHUNKS, P], F32, name="turned_sb3", align_bytes=64)
-        totals = [bank(2 + u, [P, R // 2], "total3_%d" % u) for u in range(2)]
+        totals = [bank(u, [P, R // 2], "total3_%d" % u) for u in range(2)]
         for u in range(2):
             half_term(u, right2_sb, f2, third)
             for c in (2 * u, 2 * u + 1):

@@ -42,19 +42,22 @@ def tile_picked_ynhits_val_p_kernel(
             nc.sync.dma_start(held[:], src)
             return held
 
+        def tile(name, width, dtype, on=None):
+            return sb.tile([P, width], dtype, name=name, tag=on or name, align_bytes=64)
+
         def bank(number, shape, name):
             return psum.tile(shape, F32, name=name, tag="bank%d" % number)
 
-        xs_table = sb.tile([P, T], U8, name="xs_table", align_bytes=64)
+        xs_table = tile("xs_table", T, U8)
         nc.vector.memset(xs_table[:].bitcast(I32), 0)
-        ident = sb.tile([P, P], F32, name="ident", align_bytes=64)
-        y1 = [sb.tile([P, WINDOW], F32, name="y1_%d" % t, align_bytes=64) for t in range(TILES)]
-        y2 = [sb.tile([P, WINDOW], F32, name="y2_%d" % t, align_bytes=64) for t in range(TILES)]
+        ident = tile("ident", P, F32)
+        y1 = [tile("y1_%d" % t, WINDOW, F32) for t in range(TILES)]
+        y2 = [tile("y2_%d" % t, WINDOW, F32) for t in range(TILES)]
         nc.vector.memset(ident[:], 0.0)
         make_identity(nc, ident[:], nomemset=True)
         for t in range(TILES):
             nc.vector.memset(y1[t][:, G:], 0.0)
-            nc.vector.memset(y2[t][:, W:], 0.0)
+            nc.scalar.activation(y2[t][:, W:], y1[0][:, W:], ACT.Relu)
 
         w1_rows = w1.rearrange("(p j) c -> p j c", j=PACK)
         half = H // 2
@@ -65,9 +68,10 @@ def tile_picked_ynhits_val_p_kernel(
                 xs_table[:].bitcast(I32)[32 * q : 32 * q + 4, :], x_scales[0].bitcast(I32)[4 * q : 4 * q + 4, :]
             )
         offs_sb = load_list("offs_sb", offs)
-        w1_raw[1] = load("w1_raw1", w1_rows[:, :, half:], [P, PACK, half], F32)
         xw_table = load("xw_table", x_words[0].rearrange("p n j -> p (n j)").bitcast(I32), [P, T], I32)
-        kn1_raw = load("kn1_raw", kn1.rearrange("(p j) c -> p j c", j=PACK), [P, PACK, G], F32)
+        w1_raw[1] = load("w1_raw1", w1_rows[:, :, half:], [P, PACK, half], F32)
+        kn1_rows = kn1.rearrange("(p j) c -> p j c", j=PACK)
+        kn1_raw = [load("kn1_raw%d" % u, kn1_rows[:, :, u * P : (u + 1) * P], [P, PACK, P], F32) for u in range(2)]
         right1_sb = load_list("right1_sb", right1)
         f1 = load("f1", frac1, [P, R], F32)
         left1_sb = load_list("left1_sb", left1)
@@ -77,240 +81,171 @@ def tile_picked_ynhits_val_p_kernel(
         f2 = load("f2", frac2, [P, R], F32)
         left2_sb = load_list("left2_sb", left2)
 
-        def quantize(name, grouped, width):
-            codes = sb.tile([P, width], U32, name=name + "_codes", align_bytes=64)
-            scales = sb.tile([P, width], U8, name=name + "_scales", align_bytes=64)
-            nc.vector.quantize_mx(out=codes[:].bitcast(FP8X4), scales=scales[:], in_=grouped[:])
-            return codes, scales
+        def quantize(codes, scales, grouped):
+            nc.vector.quantize_mx(out=codes.bitcast(FP8X4), scales=scales, in_=grouped)
 
-        def interleave(copy, grouped, raw, c0, c1):
+        def interleave(copy, grouped, raw):
             copy(
-                grouped[:, PACK * c0 : PACK * c1].rearrange("p (c i j) -> p c j i", i=4, j=PACK),
-                raw[:, :, c0:c1].rearrange("p j (c i) -> p c j i", i=4),
+                grouped.rearrange("p (c i j) -> p c j i", i=4, j=PACK),
+                raw.rearrange("p j (c i) -> p c j i", i=4),
             )
 
-        w1_grouped = sb.tile([P, PACK * H], BF16, name="w1_grouped", align_bytes=64)
-        w1_view = w1_grouped[:].rearrange("p (e m j) -> p m e j", e=PACK, j=PACK)
-        xg_words = sb.tile([P, S], U32, name="xg_words", align_bytes=64)
-        xg_scales = sb.tile([P, S], U8, name="xg_scales", align_bytes=64)
-
-        def gather_words(c0, c1):
-            nc.vector.tensor_copy(
-                xg_words[:, c0:c1], xw_table[:].bitcast(U32).indirect(offs_sb[:, c0 // 16 : c1 // 16])
+        def mx_pass(acc, lhs, rhs):
+            nc.tensor.matmul_mx(
+                out=acc,
+                lhsT=lhs[0].bitcast(FP8X4),
+                lhsT_scale=lhs[1],
+                rhs=rhs[0].bitcast(FP8X4),
+                rhs_scale=rhs[1],
+                start=True,
+                stop=True,
             )
 
-        nc.scalar.copy(w1_view[:, : P // 2], w1_raw[0][:].rearrange("p j (m e) -> p m e j", e=PACK))
+        w1_codes = sb.tile([P, H], U32, name="w1_codes", tag="xs_table", align_bytes=64)
+        w1_scales = tile("w1_scales", H, U8)
+        xg_words = [None] * TILES
+        xg_scales = tile("xg_scales", S, U8)
+        m_half = P // 2
+
+        def cast_w1(copy, u, e0, e1):
+            grouped = tile("w1_grouped%d_%d" % (u, e0), (e1 - e0) * m_half * PACK, BF16)
+            copy(
+                grouped[:].rearrange("p (e m j) -> p m e j", m=m_half, j=PACK),
+                w1_raw[u][:].rearrange("p j (m e) -> p m e j", e=PACK)[:, :, e0:e1, :],
+            )
+            return grouped
+
+        def quantize_w1(grouped, u, e0, e1):
+            for e in range(e0, e1):
+                cols = slice(e * P + u * m_half, e * P + (u + 1) * m_half)
+                width = m_half * PACK
+                quantize(w1_codes[:, cols], w1_scales[:, cols], grouped[:, (e - e0) * width : (e - e0 + 1) * width])
+
+        def gather_words(t0, t1, on=None):
+            picked = tile("xg_words%d" % t0, (t1 - t0) * P, U32, on)
+            nc.vector.tensor_copy(picked[:], xw_table[:].bitcast(U32).indirect(offs_sb[:, t0 * P // 16 : t1 * P // 16]))
+            for t in range(t0, t1):
+                xg_words[t] = picked[:, (t - t0) * P : (t - t0 + 1) * P]
+
+        first_half = cast_w1(nc.scalar.copy, 0, 0, PACK)
         nc.vector.tensor_copy(xg_scales[:], xs_table[:].indirect(offs_sb[:]))
-        nc.vector.tensor_copy(w1_view[:, P // 2 :], w1_raw[1][:].rearrange("p j (m e) -> p m e j", e=PACK))
-        w1_codes, w1_scales = quantize("w1", w1_grouped, H)
-        gather_words(0, P)
-        gather_words(P, 2 * P)
+        gather_words(0, 1)
+        quantize_w1(first_half, 0, 0, PACK)
+        on_vector = cast_w1(nc.vector.tensor_copy, 1, 0, 2)
+        on_scalar = cast_w1(nc.scalar.copy, 1, 2, PACK)
+        quantize_w1(on_vector, 1, 0, 2)
+        quantize_w1(on_scalar, 1, 2, PACK)
+        gather_words(1, 2, on="w1_grouped1_2")
 
         def hidden(number, t):
             cols = slice(t * P, (t + 1) * P)
             acc = bank(number, [P, PACK, P], "h_acc%d" % t)
             for e in range(PACK):
                 ch = slice(e * P, (e + 1) * P)
-                nc.tensor.matmul_mx(
-                    out=acc[:, e, :],
-                    lhsT=w1_codes[:, ch].bitcast(FP8X4),
-                    lhsT_scale=w1_scales[:, ch],
-                    rhs=xg_words[:, cols].bitcast(FP8X4),
-                    rhs_scale=xg_scales[:, cols],
-                    start=True,
-                    stop=True,
-                )
-            grouped = sb.tile([P, PACK * P], BF16, name="h_grouped%d" % t, align_bytes=64)
+                mx_pass(acc[:, e, :], (w1_codes[:, ch], w1_scales[:, ch]), (xg_words[t], xg_scales[:, cols]))
+            grouped = tile("h_grouped%d" % t, PACK * P, BF16)
             nc.scalar.activation(
                 grouped[:].rearrange("p (n e) -> p n e", e=PACK), acc[:].rearrange("p e n -> p n e"), ACT.Relu
             )
-            return quantize("h%d" % t, grouped, P)
+            codes = tile("h_codes%d" % t, P, U32)
+            scales = tile("h_scales%d" % t, P, U8)
+            quantize(codes[:], scales[:], grouped[:])
+            return codes[:], scales[:]
 
         def knots(number, h, kn, window, width, name):
             acc = bank(number, [P, width], name)
-            nc.tensor.matmul_mx(
-                out=acc[:],
-                lhsT=h[0][:].bitcast(FP8X4),
-                lhsT_scale=h[1][:],
-                rhs=kn[0][:].bitcast(FP8X4),
-                rhs_scale=kn[1][:],
-                start=True,
-                stop=True,
-            )
+            mx_pass(acc[:], h, kn)
             nc.scalar.copy(window[:, :width], acc[:])
 
-        kn1_grouped = sb.tile([P, PACK * G], BF16, name="kn1_grouped", align_bytes=64)
-        kn1_codes = sb.tile([P, G], U32, name="kn1_codes", align_bytes=64)
-        kn1_scales = sb.tile([P, G], U8, name="kn1_scales", align_bytes=64)
-        kn1_q = (kn1_codes, kn1_scales)
-        for c0 in range(0, G, P):
-            interleave(nc.vector.tensor_copy, kn1_grouped, kn1_raw, c0, c0 + P)
-        for c0 in range(0, G, P):
-            nc.vector.quantize_mx(
-                out=kn1_codes[:, c0 : c0 + P].bitcast(FP8X4),
-                scales=kn1_scales[:, c0 : c0 + P],
-                in_=kn1_grouped[:, PACK * c0 : PACK * (c0 + P)],
-            )
+        kn1_codes = tile("kn1_codes", G, U32)
+        kn1_scales = tile("kn1_scales", G, U8)
+        kn1_q = (kn1_codes[:], kn1_scales[:])
+        kn1_grouped = tile("kn1_grouped", PACK * G, BF16)
+        for u, copy in enumerate((nc.scalar.copy, nc.vector.tensor_copy)):
+            interleave(copy, kn1_grouped[:, u * PACK * P : (u + 1) * PACK * P], kn1_raw[u][:])
+        gather_words(2, 3, on="kn1_raw1")
+        quantize(kn1_codes[:], kn1_scales[:], kn1_grouped[:])
         hq = [None] * TILES
         hq[0] = hidden(0, 0)
-        knots(2, hq[0], kn1_q, y1[0], G, "y1_acc0")
-        gather_words(2 * P, S)
-        a1 = sb.tile([P, R], F32, name="a1", tag="h_grouped0", align_bytes=64)
-        nc.vector.tensor_scalar(a1[:], f1[:], -1.0, 1.0, ALU.mult, ALU.add)
+        gather_words(3, TILES, on="h_grouped0")
         hq[1] = hidden(1, 1)
+        knots(2, hq[0], kn1_q, y1[0], G, "y1_acc0")
+        a1 = tile("a1", R, F32, on="h_grouped1")
+        nc.vector.tensor_scalar(a1[:], f1[:], -1.0, 1.0, ALU.mult, ALU.add)
         knots(3, hq[1], kn1_q, y1[1], G, "y1_acc1")
+        hq[2] = hidden(2, 2)
 
-        kn2_codes = sb.tile([P, W], U32, name="kn2_codes", align_bytes=64)
-        kn2_scales = sb.tile([P, W], U8, name="kn2_scales", align_bytes=64)
-        kn2_q = (kn2_codes, kn2_scales)
-        for u in range(2):
-            cols = slice(u * G, (u + 1) * G)
-            grouped = sb.tile([P, PACK * G], BF16, name="kn2_grouped%d" % u, align_bytes=64)
-            for c0 in range(0, G, P):
-                interleave(nc.scalar.copy, grouped, kn2_raw[u], c0, c0 + P)
-            nc.vector.quantize_mx(out=kn2_codes[:, cols].bitcast(FP8X4), scales=kn2_scales[:, cols], in_=grouped[:])
-            knots(u, hq[0], (kn2_codes[:, cols], kn2_scales[:, cols]), y2[0][:, cols], G, "y2_acc0_%d" % u)
-        after_casts = sb.tile([P, 2 * R + R // 2], F32, name="after_casts", tag="kn2_raw1", align_bytes=64)
-        a2 = after_casts[:, :R]
-        nc.scalar.activation(a2, f2[:], ACT.Copy, bias=1.0, scale=-1.0)
-        knots(0, hq[1], kn2_q, y2[1], W, "y2_acc1")
-        hq[2] = hidden(1, 2)
-        hq[3] = hidden(0, 3)
-        knots(1, hq[2], kn1_q, y1[2], G, "y1_acc2")
+        kn2_codes = tile("kn2_codes", W, U32)
+        kn2_scales = tile("kn2_scales", W, U8)
+        kn2_q = (kn2_codes[:], kn2_scales[:])
+        kn2_grouped = tile("kn2_grouped", PACK * W, BF16)
+        for c0 in range(0, W, P):
+            raw = kn2_raw[c0 // G][:, :, c0 % G : c0 % G + P]
+            interleave(nc.scalar.copy, kn2_grouped[:, PACK * c0 : PACK * (c0 + P)], raw)
+        quantize(kn2_codes[:], kn2_scales[:], kn2_grouped[:])
+        knots(0, hq[2], kn1_q, y1[2], G, "y1_acc2")
+        hq[3] = hidden(3, 3)
+        a2 = tile("a2", R, F32)
+        nc.scalar.activation(a2[:], f2[:], ACT.Copy, bias=1.0, scale=-1.0)
+        knots(1, hq[0], kn2_q, y2[0], W, "y2_acc0")
+        knots(2, hq[1], kn2_q, y2[1], W, "y2_acc1")
         knots(0, hq[2], kn2_q, y2[2], W, "y2_acc2")
-        knots(0, hq[3], kn1_q, y1[3], G, "y1_acc3")
+        knots(1, hq[3], kn1_q, y1[3], G, "y1_acc3")
+        knots(2, hq[3], kn2_q, y2[3], W, "y2_acc3")
 
-        terms = [[] for t in range(TILES)]
-
-        def product_tile(name, tag, width=R):
-            return sb.tile([P, width], F32, name=name, tag=tag, align_bytes=64)
-
-        def term(t, window, offsets, weight, product):
-            nc.vector.tensor_tensor(product, window[:].indirect(offsets[:]), weight[:], ALU.mult)
-            terms[t].append(product)
-
-        def r1(t, product=None):
-            term(t, y1[t], right1_sb, f1, product_tile("r1_%d" % t, "r1_%d" % t)[:] if product is None else product)
-
-        def l1(t, product=None):
-            term(t, y1[t], left1_sb, a1, product_tile("l1_%d" % t, "l1_%d" % t)[:] if product is None else product)
-
-        def r2(t, product=None):
-            term(t, y2[t], right2_sb, f2, product_tile("r2_%d" % t, "r2_%d" % t)[:] if product is None else product)
-
-        def l2(t, product=None):
-            term(t, y2[t], left2_sb, a2, product_tile("l2_%d" % t, "l2_%d" % t)[:] if product is None else product)
-
-        def turn(turned, part, c, first, last):
-            nc.tensor.matmul(
-                turned, lhsT=part[:, c * P : (c + 1) * P], rhs=ident[:], start=first, stop=last, is_transpose=True
+        def term(name, window, offsets, weight, c0=0, c1=R):
+            product = tile(name, c1 - c0, F32)
+            nc.vector.tensor_tensor(
+                product[:], window[:].indirect(offsets[:, c0 // 16 : c1 // 16]), weight[:, c0:c1], ALU.mult
             )
+            return product
 
-        def tensor_sum(t, forward, back):
-            turned = bank(forward, [P, CHUNKS, P], "turned%d" % t)
-            parts = list(terms[t])
-            for c in range(CHUNKS):
-                for i, part in enumerate(parts):
-                    turn(turned[:, c, :], part, c, i == 0, i == len(parts) - 1)
-            turned_sb = sb.tile([P, CHUNKS, P], F32, name="turned_sb%d" % t, align_bytes=64)
+        def add_turned(turned, part, first, last):
+            chunks = turned.shape[1]
+            for c in range(chunks):
+                nc.tensor.matmul(
+                    turned[:, c, :],
+                    lhsT=part[:, c * P : (c + 1) * P],
+                    rhs=ident[:],
+                    start=first and c == 0,
+                    stop=last and c == chunks - 1,
+                    is_transpose=True,
+                )
+
+        def turn_back(turned, number, name):
+            chunks = turned.shape[1]
+            turned_sb = sb.tile([P, chunks, P], F32, name=name + "_turned", align_bytes=64)
             nc.scalar.copy(turned_sb[:], turned[:])
-            total = bank(back, [P, R], "total%d" % t)
-            for c in range(CHUNKS):
+            total = bank(number, [P, chunks * P], name + "_total")
+            for c in range(chunks):
                 nc.tensor.transpose(total[:, c * P : (c + 1) * P], turned_sb[:, c, :], ident[:])
             return total
 
-        def open_banks(t, numbers):
-            return [bank(n, [P, P], "turned%d_%d" % (t, c)) for c, n in enumerate(numbers)]
-
-        def add_latest(t, banks, first=False, last=False):
-            for c in range(CHUNKS):
-                turn(banks[c][:], terms[t][-1], c, first, last)
-
-        def turn_back(t, banks, back):
-            turned_sb = sb.tile([P, CHUNKS, P], F32, name="turned_sb%d" % t, align_bytes=64)
-            total = bank(back, [P, R], "total%d" % t)
-            for c in range(CHUNKS):
-                nc.scalar.copy(turned_sb[:, c, :], banks[c][:])
-                nc.tensor.transpose(total[:, c * P : (c + 1) * P], turned_sb[:, c, :], ident[:])
-            return total
-
-        def store(t, result):
+        last = TILES - 1
+        turned = [bank(4 + t, [P, CHUNKS, P], "turned%d" % t) for t in range(last)]
+        for t in range(last):
+            add_turned(turned[t], term("r1_%d" % t, y1[t], right1_sb, f1), True, False)
+            add_turned(turned[t], term("l1_%d" % t, y1[t], left1_sb, a1), False, False)
+        for t, back in enumerate((3, 0, 1)):
+            add_turned(turned[t], term("r2_%d" % t, y2[t], right2_sb, f2), False, False)
+            add_turned(turned[t], term("l2_%d" % t, y2[t], left2_sb, a2), False, True)
+            total = turn_back(turned[t], back, "sum%d" % t)
+            result = tile("result%d" % t, R, F32)
+            nc.scalar.copy(result[:], total[:])
             nc.sync.dma_start(out[t * P : (t + 1) * P, :], result[:])
 
-        def finish_on_scalar(t, total):
-            result = sb.tile([P, R], F32, name="result%d" % t, align_bytes=64)
-            nc.scalar.copy(result[:], total[:])
-            store(t, result)
-
-        def finish_on_vector(t, total):
-            result = sb.tile([P, R], F32, name="result%d" % t, align_bytes=64)
-            nc.vector.tensor_tensor(result[:], total[:], terms[t][3], ALU.add)
-            store(t, result)
-
-        banks0 = open_banks(0, [4, 5, 6, 7])
-        r1(0)
-        add_latest(0, banks0, first=True)
-        l1(0)
-        add_latest(0, banks0)
-        banks1 = [bank(2 + c, [P, P], "turned1_%d" % c) for c in range(2)]
-        r1_halves = [product_tile("r1_1", "kn2_raw0", R // 2)[:], after_casts[:, 2 * R :]]
-        for u in range(2):
-            nc.vector.tensor_tensor(
-                r1_halves[u],
-                y1[1][:].indirect(right1_sb[:, u * 16 : (u + 1) * 16]),
-                f1[:, u * R // 2 : (u + 1) * R // 2],
-                ALU.mult,
-            )
-        for c in range(2):
-            turn(banks1[c][:], r1_halves[0], c, True, False)
-        l1(1, after_casts[:, R : 2 * R])
-        for c in range(2):
-            turn(banks1[c][:], terms[1][0], c, False, False)
-        r2(0)
-        add_latest(0, banks0)
-        l2(0)
-        add_latest(0, banks0, last=True)
-        finish_on_scalar(0, turn_back(0, banks0, 1))
-        knots(1, hq[3], kn2_q, y2[3], W, "y2_acc3")
-        banks1 = banks1 + [bank(2 + c, [P, P], "turned1_%d" % c) for c in range(2, 4)]
-        for c in range(2, 4):
-            turn(banks1[c][:], r1_halves[1], c - 2, True, False)
-            turn(banks1[c][:], terms[1][0], c, False, False)
-        r2(1)
-        add_latest(1, banks1)
-        l2(1)
-        add_latest(1, banks1, last=True)
-        finish_on_scalar(1, turn_back(1, banks1, 0))
-        banks2 = open_banks(2, [6, 7, 2, 3])
-        for i, gather in enumerate((r1, l1, r2, l2)):
-            gather(2)
-            add_latest(2, banks2, first=(i == 0), last=(i == 3))
-        finish_on_scalar(2, turn_back(2, banks2, 1))
-        banks3 = open_banks(3, [4, 5, 6, 7])
-        for i, gather in enumerate((r1, l1)):
-            gather(3)
-            add_latest(3, banks3, first=(i == 0))
-        halves = [slice(u * R // 2, (u + 1) * R // 2) for u in range(2)]
-
-        def half_term(u, offsets, weight, product):
-            nc.vector.tensor_tensor(
-                product[:, halves[u]], y2[3][:].indirect(offsets[:, u * 16 : (u + 1) * 16]), weight[:, halves[u]], ALU.mult
-            )
-
-        third = product_tile("r2_3", "r2_3")
-        last = product_tile("l2_3", "l2_3")
-        turned_sb = sb.tile([P, CHUNKS, P], F32, name="turned_sb3", align_bytes=64)
-        totals = [bank(u, [P, R // 2], "total3_%d" % u) for u in range(2)]
-        for u in range(2):
-            half_term(u, right2_sb, f2, third)
-            for c in (2 * u, 2 * u + 1):
-                turn(banks3[c][:], third, c, False, True)
-            for c in (2 * u, 2 * u + 1):
-                nc.scalar.copy(turned_sb[:, c, :], banks3[c][:])
-                nc.tensor.transpose(totals[u][:, (c % 2) * P : (c % 2 + 1) * P], turned_sb[:, c, :], ident[:])
-        for u in range(2):
-            half_term(u, left2_sb, a2, last)
-        for u, cols in enumerate(halves):
-            result = sb.tile([P, R // 2], F32, name="result3_%d" % u, align_bytes=64)
-            nc.vector.tensor_tensor(result[:], totals[u][:], last[:, cols], ALU.add)
-            nc.sync.dma_start(out[3 * P :, cols], result[:])
+        halves = [(u * R // 2, (u + 1) * R // 2) for u in range(2)]
+        turned_last = [bank(number, [P, CHUNKS // 2, P], "turned_last%d" % number) for number in (7, 4)]
+        for i, (offsets, weight) in enumerate(((right1_sb, f1), (left1_sb, a1))):
+            part = term("first_rate%d" % i, y1[last], offsets, weight)
+            for u, (c0, c1) in enumerate(halves):
+                add_turned(turned_last[u], part[:, c0:c1], i == 0, False)
+        totals = []
+        for u, (c0, c1) in enumerate(halves):
+            add_turned(turned_last[u], term("r2_last%d" % u, y2[last], right2_sb, f2, c0, c1), False, True)
+            totals.append(turn_back(turned_last[u], 2 + u, "sum_last%d" % u))
+        closing = [term("l2_last%d" % u, y2[last], left2_sb, a2, c0, c1) for u, (c0, c1) in enumerate(halves)]
+        for u, (c0, c1) in enumerate(halves):
+            result = tile("result_last%d" % u, c1 - c0, F32)
+            nc.vector.tensor_tensor(result[:], totals[u][:], closing[u][:], ALU.add)
+            nc.sync.dma_start(out[last * P :, c0:c1], result[:])

@@ -70,8 +70,7 @@ def tile_picked_ynhits_val_p_kernel(
         offs_sb = load_list("offs_sb", offs)
         xw_table = load("xw_table", x_words[0].rearrange("p n j -> p (n j)").bitcast(I32), [P, T], I32)
         w1_raw[1] = load("w1_raw1", w1_rows[:, :, half:], [P, PACK, half], F32)
-        kn1_rows = kn1.rearrange("(p j) c -> p j c", j=PACK)
-        kn1_raw = [load("kn1_raw%d" % u, kn1_rows[:, :, u * P : (u + 1) * P], [P, PACK, P], F32) for u in range(2)]
+        kn1_raw = load("kn1_raw", kn1.rearrange("(p j) c -> p j c", j=PACK), [P, PACK, G], F32)
         right1_sb = load_list("right1_sb", right1)
         f1 = load("f1", frac1, [P, R], F32)
         left1_sb = load_list("left1_sb", left1)
@@ -161,13 +160,14 @@ def tile_picked_ynhits_val_p_kernel(
         kn1_scales = tile("kn1_scales", G, U8)
         kn1_q = (kn1_codes[:], kn1_scales[:])
         kn1_grouped = tile("kn1_grouped", PACK * G, BF16)
-        for u, copy in enumerate((nc.scalar.copy, nc.vector.tensor_copy)):
-            interleave(copy, kn1_grouped[:, u * PACK * P : (u + 1) * PACK * P], kn1_raw[u][:])
-        gather_words(2, 3, on="kn1_raw1")
-        quantize(kn1_codes[:], kn1_scales[:], kn1_grouped[:])
+        for c0 in range(0, G, P):
+            interleave(nc.vector.tensor_copy, kn1_grouped[:, PACK * c0 : PACK * (c0 + P)], kn1_raw[:, :, c0 : c0 + P])
+        for c0 in range(0, G, P):
+            cols = slice(c0, c0 + P)
+            quantize(kn1_codes[:, cols], kn1_scales[:, cols], kn1_grouped[:, PACK * c0 : PACK * (c0 + P)])
         hq = [None] * TILES
         hq[0] = hidden(0, 0)
-        gather_words(3, TILES, on="h_grouped0")
+        gather_words(2, TILES, on="h_grouped0")
         hq[1] = hidden(1, 1)
         knots(2, hq[0], kn1_q, y1[0], G, "y1_acc0")
         a1 = tile("a1", R, F32, on="h_grouped1")
@@ -193,8 +193,8 @@ def tile_picked_ynhits_val_p_kernel(
         knots(1, hq[3], kn1_q, y1[3], G, "y1_acc3")
         knots(2, hq[3], kn2_q, y2[3], W, "y2_acc3")
 
-        def term(name, window, offsets, weight, c0=0, c1=R):
-            product = tile(name, c1 - c0, F32)
+        def term(name, window, offsets, weight, c0=0, c1=R, on=None):
+            product = tile(name, c1 - c0, F32, on)
             nc.vector.tensor_tensor(
                 product[:], window[:].indirect(offsets[:, c0 // 16 : c1 // 16]), weight[:, c0:c1], ALU.mult
             )
@@ -224,7 +224,8 @@ def tile_picked_ynhits_val_p_kernel(
         last = TILES - 1
         turned = [bank(4 + t, [P, CHUNKS, P], "turned%d" % t) for t in range(last)]
         for t in range(last):
-            add_turned(turned[t], term("r1_%d" % t, y1[t], right1_sb, f1), True, False)
+            on = "kn2_raw1" if t == last - 1 else None
+            add_turned(turned[t], term("r1_%d" % t, y1[t], right1_sb, f1, on=on), True, False)
             add_turned(turned[t], term("l1_%d" % t, y1[t], left1_sb, a1), False, False)
         for t, back in enumerate((3, 0, 1)):
             add_turned(turned[t], term("r2_%d" % t, y2[t], right2_sb, f2), False, False)
@@ -232,20 +233,24 @@ def tile_picked_ynhits_val_p_kernel(
             total = turn_back(turned[t], back, "sum%d" % t)
             result = tile("result%d" % t, R, F32)
             nc.scalar.copy(result[:], total[:])
-            nc.sync.dma_start(out[t * P : (t + 1) * P, :], result[:])
+            nc.scalar.dma_start(out[t * P : (t + 1) * P, :], result[:])
 
-        halves = [(u * R // 2, (u + 1) * R // 2) for u in range(2)]
-        turned_last = [bank(number, [P, CHUNKS // 2, P], "turned_last%d" % number) for number in (7, 4)]
-        for i, (offsets, weight) in enumerate(((right1_sb, f1), (left1_sb, a1))):
-            part = term("first_rate%d" % i, y1[last], offsets, weight)
-            for u, (c0, c1) in enumerate(halves):
-                add_turned(turned_last[u], part[:, c0:c1], i == 0, False)
-        totals = []
-        for u, (c0, c1) in enumerate(halves):
-            add_turned(turned_last[u], term("r2_last%d" % u, y2[last], right2_sb, f2, c0, c1), False, True)
-            totals.append(turn_back(turned_last[u], 2 + u, "sum_last%d" % u))
-        closing = [term("l2_last%d" % u, y2[last], left2_sb, a2, c0, c1) for u, (c0, c1) in enumerate(halves)]
-        for u, (c0, c1) in enumerate(halves):
-            result = tile("result_last%d" % u, c1 - c0, F32)
-            nc.vector.tensor_tensor(result[:], totals[u][:], closing[u][:], ALU.add)
-            nc.sync.dma_start(out[last * P :, c0:c1], result[:])
+        half_r = R // 2
+        turned_last = bank(4 + last - 1, [P, CHUNKS // 2, P], "turned_last")
+        right_first = term("r1_last", y1[last], right1_sb, f1)
+        add_turned(turned_last, right_first[:, :half_r], True, False)
+        left_first = term("l1_last", y1[last], left1_sb, a1)
+        add_turned(turned_last, left_first[:, :half_r], False, False)
+        add_turned(turned_last, term("r2_last0", y2[last], right2_sb, f2, 0, half_r), False, True)
+        lower = turn_back(turned_last, 2, "sum_last")
+        right_second = term("r2_last1", y2[last], right2_sb, f2, half_r, R)
+        two = tile("two_terms", half_r, F32)
+        nc.vector.tensor_tensor(two[:], right_first[:, half_r:], left_first[:, half_r:], ALU.add)
+        closing_upper = term("l2_last1", y2[last], left2_sb, a2, half_r, R)
+        upper = tile("three_terms", half_r, F32)
+        nc.vector.tensor_tensor(upper[:], two[:], right_second[:], ALU.add)
+        closing_lower = term("l2_last0", y2[last], left2_sb, a2, 0, half_r)
+        for c0, three, closing in ((half_r, upper, closing_upper), (0, lower, closing_lower)):
+            result = tile("result_last%d" % c0, half_r, F32)
+            nc.vector.tensor_tensor(result[:], three[:], closing[:], ALU.add)
+            nc.sync.dma_start(out[last * P :, c0 : c0 + half_r], result[:])

@@ -215,10 +215,11 @@ def tile_picked_ynhits_val_p_kernel(
         def turn_back(turned, number, name):
             chunks = turned.shape[1]
             turned_sb = sb.tile([P, chunks, P], F32, name=name + "_turned", align_bytes=64)
-            nc.scalar.copy(turned_sb[:], turned[:])
             total = bank(number, [P, chunks * P], name + "_total")
-            for c in range(chunks):
-                nc.tensor.transpose(total[:, c * P : (c + 1) * P], turned_sb[:, c, :], ident[:])
+            for c0 in range(0, chunks, 2):
+                nc.scalar.copy(turned_sb[:, c0 : c0 + 2, :], turned[:, c0 : c0 + 2, :])
+                for c in (c0, c0 + 1):
+                    nc.tensor.transpose(total[:, c * P : (c + 1) * P], turned_sb[:, c, :], ident[:])
             return total
 
         last = TILES - 1
@@ -235,22 +236,23 @@ def tile_picked_ynhits_val_p_kernel(
             nc.scalar.copy(result[:], total[:])
             nc.scalar.dma_start(out[t * P : (t + 1) * P, :], result[:])
 
-        half_r = R // 2
-        turned_last = bank(4 + last - 1, [P, CHUNKS // 2, P], "turned_last")
-        right_first = term("r1_last", y1[last], right1_sb, f1)
-        add_turned(turned_last, right_first[:, :half_r], True, False)
-        left_first = term("l1_last", y1[last], left1_sb, a1)
-        add_turned(turned_last, left_first[:, :half_r], False, False)
-        add_turned(turned_last, term("r2_last0", y2[last], right2_sb, f2, 0, half_r), False, True)
-        lower = turn_back(turned_last, 2, "sum_last")
-        right_second = term("r2_last1", y2[last], right2_sb, f2, half_r, R)
-        two = tile("two_terms", half_r, F32)
-        nc.vector.tensor_tensor(two[:], right_first[:, half_r:], left_first[:, half_r:], ALU.add)
-        closing_upper = term("l2_last1", y2[last], left2_sb, a2, half_r, R)
-        upper = tile("three_terms", half_r, F32)
-        nc.vector.tensor_tensor(upper[:], two[:], right_second[:], ALU.add)
-        closing_lower = term("l2_last0", y2[last], left2_sb, a2, 0, half_r)
-        for c0, three, closing in ((half_r, upper, closing_upper), (0, lower, closing_lower)):
-            result = tile("result_last%d" % c0, half_r, F32)
-            nc.vector.tensor_tensor(result[:], three[:], closing[:], ALU.add)
-            nc.sync.dma_start(out[last * P :, c0 : c0 + half_r], result[:])
+        halves = [(u * R // 2, (u + 1) * R // 2) for u in range(2)]
+        turned_last = [bank(number, [P, 1, P], "turned_last%d" % number) for number in (6, 7, 4, 5)]
+        for i, (offsets, weight) in enumerate(((right1_sb, f1), (left1_sb, a1))):
+            part = term("first_rate%d" % i, y1[last], offsets, weight)
+            for c in range(CHUNKS):
+                add_turned(turned_last[c], part[:, c * P : (c + 1) * P], i == 0, False)
+        totals = [bank(2 + u, [P, R // 2], "total_last%d" % u) for u in range(2)]
+        for first, count in ((0, 2), (2, 1), (3, 1)):
+            part = term("r2_last%d" % first, y2[last], right2_sb, f2, first * P, (first + count) * P)
+            for c in range(count):
+                add_turned(turned_last[first + c], part[:, c * P : (c + 1) * P], False, True)
+            for c in range(first, first + count):
+                turned_sb = tile("turned_sb%d" % c, P, F32)
+                nc.scalar.copy(turned_sb[:], turned_last[c][:, 0, :])
+                nc.tensor.transpose(totals[c // 2][:, (c % 2) * P : (c % 2 + 1) * P], turned_sb[:], ident[:])
+        closing = [term("l2_last%d" % u, y2[last], left2_sb, a2, c0, c1) for u, (c0, c1) in enumerate(halves)]
+        for u, (c0, c1) in enumerate(halves):
+            result = tile("result_last%d" % u, c1 - c0, F32)
+            nc.vector.tensor_tensor(result[:], totals[u][:], closing[u][:], ALU.add)
+            nc.sync.dma_start(out[last * P :, c0:c1], result[:])

@@ -109,8 +109,8 @@ def tile_picked_ynhits_val_p_kernel(
         def cast_w1(copy, u, e0, e1):
             grouped = tile("w1_grouped%d_%d" % (u, e0), (e1 - e0) * m_half * PACK, BF16)
             copy(
-                grouped[:].rearrange("p (e m j) -> p m e j", m=m_half, j=PACK),
-                w1_raw[u][:].rearrange("p j (m e) -> p m e j", e=PACK)[:, :, e0:e1, :],
+                grouped[:].rearrange("p (e m j) -> p m j e", m=m_half, j=PACK),
+                w1_raw[u][:].rearrange("p j (m e) -> p m j e", e=PACK)[:, :, :, e0:e1],
             )
             return grouped
 

@@ -236,23 +236,31 @@ def tile_picked_ynhits_val_p_kernel(
             nc.scalar.copy(result[:], total[:])
             nc.scalar.dma_start(out[t * P : (t + 1) * P, :], result[:])
 
-        halves = [(u * R // 2, (u + 1) * R // 2) for u in range(2)]
+        pieces = [(0, 2), (2, 3), (3, CHUNKS)]
         turned_last = [bank(number, [P, 1, P], "turned_last%d" % number) for number in (6, 7, 4, 5)]
-        for i, (offsets, weight) in enumerate(((right1_sb, f1), (left1_sb, a1))):
-            part = term("first_rate%d" % i, y1[last], offsets, weight)
-            for c in range(CHUNKS):
-                add_turned(turned_last[c], part[:, c * P : (c + 1) * P], i == 0, False)
-        totals = [bank(2 + u, [P, R // 2], "total_last%d" % u) for u in range(2)]
-        for first, count in ((0, 2), (2, 1), (3, 1)):
-            part = term("r2_last%d" % first, y2[last], right2_sb, f2, first * P, (first + count) * P)
-            for c in range(count):
-                add_turned(turned_last[first + c], part[:, c * P : (c + 1) * P], False, True)
-            for c in range(first, first + count):
+        totals = [bank(number, [P, (c1 - c0) * P], "total_last%d" % c0) for number, (c0, c1) in zip((2, 3, 0), pieces)]
+
+        def add_chunks(part, c0, c1, first, closes):
+            for c in range(c0, c1):
+                add_turned(turned_last[c], part[:, (c - c0) * P : (c - c0 + 1) * P], first, closes)
+
+        def third_term(number):
+            c0, c1 = pieces[number]
+            add_chunks(term("r2_last%d" % c0, y2[last], right2_sb, f2, c0 * P, c1 * P), c0, c1, False, True)
+            for c in range(c0, c1):
                 turned_sb = tile("turned_sb%d" % c, P, F32)
                 nc.scalar.copy(turned_sb[:], turned_last[c][:, 0, :])
-                nc.tensor.transpose(totals[c // 2][:, (c % 2) * P : (c % 2 + 1) * P], turned_sb[:], ident[:])
-        closing = [term("l2_last%d" % u, y2[last], left2_sb, a2, c0, c1) for u, (c0, c1) in enumerate(halves)]
-        for u, (c0, c1) in enumerate(halves):
-            result = tile("result_last%d" % u, c1 - c0, F32)
-            nc.vector.tensor_tensor(result[:], totals[u][:], closing[u][:], ALU.add)
-            nc.sync.dma_start(out[last * P :, c0:c1], result[:])
+                nc.tensor.transpose(totals[number][:, (c - c0) * P : (c - c0 + 1) * P], turned_sb[:], ident[:])
+
+        add_chunks(term("r1_last", y1[last], right1_sb, f1), 0, CHUNKS, True, False)
+        add_chunks(term("l1_last0", y1[last], left1_sb, a1, 0, 2 * P), 0, 2, False, False)
+        third_term(0)
+        add_chunks(term("l1_last2", y1[last], left1_sb, a1, 2 * P, R), 2, CHUNKS, False, False)
+        third_term(1)
+        third_term(2)
+        closing = [term("l2_last%d" % c0, y2[last], left2_sb, a2, c0, c0 + 2 * P) for c0 in (0, 2 * P)]
+        for total, (c0, c1) in zip(totals, pieces):
+            result = tile("result_last%d" % c0, (c1 - c0) * P, F32)
+            fourth = closing[c0 // 2][:, (c0 % 2) * P : (c0 % 2 + c1 - c0) * P]
+            nc.vector.tensor_tensor(result[:], total[:], fourth, ALU.add)
+            nc.sync.dma_start(out[last * P :, c0 * P : c1 * P], result[:])

@@ -21,6 +21,8 @@ PACK = 4
 TILES = S // P
 CHUNKS = R // P
 WINDOW = R + 16
+TURN_BANKS = (4, 5, 6, 7)
+BACK_BANKS = (0, 1, 2, 3)
 
 
 def tile_picked_ynhits_val_p_kernel(
@@ -30,6 +32,7 @@ def tile_picked_ynhits_val_p_kernel(
     with ExitStack() as ctx:
         lists = ctx.enter_context(tc.tile_pool(name="lists", bufs=1))
         sb = ctx.enter_context(tc.tile_pool(name="sb", bufs=1))
+        laid = ctx.enter_context(tc.tile_pool(name="laid", bufs=1))
         psum = ctx.enter_context(tc.psum_pool(name="psum", bufs=1))
 
         def load_list(name, src):
@@ -45,8 +48,7 @@ def tile_picked_ynhits_val_p_kernel(
         def tile(name, width, dtype, on=None):
             return sb.tile([P, width], dtype, name=name, tag=on or name, align_bytes=64)
 
-        def bank(number, shape, name):
-            return psum.tile(shape, F32, name=name, tag="bank%d" % number)
+        banks = [psum.tile([P, R], F32, name="bank%d" % number) for number in range(8)]
 
         xs_table = tile("xs_table", T, U8)
         nc.vector.memset(xs_table[:].bitcast(I32), 0)
@@ -71,14 +73,14 @@ def tile_picked_ynhits_val_p_kernel(
         xw_table = load("xw_table", x_words[0].rearrange("p n j -> p (n j)").bitcast(I32), [P, T], I32)
         w1_raw[1] = load("w1_raw1", w1_rows[:, :, half:], [P, PACK, half], F32)
         kn1_raw = load("kn1_raw", kn1.rearrange("(p j) c -> p j c", j=PACK), [P, PACK, G], F32)
-        right1_sb = load_list("right1_sb", right1)
-        f1 = load("f1", frac1, [P, R], F32)
         left1_sb = load_list("left1_sb", left1)
         kn2_rows = kn2.rearrange("(p j) c -> p j c", j=PACK)
         kn2_raw = [load("kn2_raw%d" % u, kn2_rows[:, :, u * G : (u + 1) * G], [P, PACK, G], F32) for u in range(2)]
+        right1_sb = load_list("right1_sb", right1)
+        f1 = load("f1", frac1, [P, R], F32)
+        left2_sb = load_list("left2_sb", left2)
         right2_sb = load_list("right2_sb", right2)
         f2 = load("f2", frac2, [P, R], F32)
-        left2_sb = load_list("left2_sb", left2)
 
         def quantize(codes, scales, grouped):
             nc.vector.quantize_mx(out=codes.bitcast(FP8X4), scales=scales, in_=grouped)
@@ -136,25 +138,26 @@ def tile_picked_ynhits_val_p_kernel(
         quantize_w1(on_scalar, 1, 2, PACK)
         gather_words(1, 2, on="w1_grouped1_2")
 
-        def hidden(number, t):
+        def hidden(number, t, grouped=None, codes=None):
             cols = slice(t * P, (t + 1) * P)
-            acc = bank(number, [P, PACK, P], "h_acc%d" % t)
+            acc = banks[number][:].rearrange("p (e n) -> p e n", e=PACK)
             for e in range(PACK):
                 ch = slice(e * P, (e + 1) * P)
                 mx_pass(acc[:, e, :], (w1_codes[:, ch], w1_scales[:, ch]), (xg_words[t], xg_scales[:, cols]))
-            grouped = tile("h_grouped%d" % t, PACK * P, BF16)
-            nc.scalar.activation(
-                grouped[:].rearrange("p (n e) -> p n e", e=PACK), acc[:].rearrange("p e n -> p n e"), ACT.Relu
-            )
-            codes = tile("h_codes%d" % t, P, U32)
+            if grouped is None:
+                held = tile("h_grouped%d" % t, PACK * P, BF16)
+                grouped = held[:]
+            nc.scalar.activation(grouped.rearrange("p (n e) -> p n e", e=PACK), acc.rearrange("p e n -> p n e"), ACT.Relu)
+            if codes is None:
+                codes = tile("h_codes%d" % t, P, U32)
             scales = tile("h_scales%d" % t, P, U8)
-            quantize(codes[:], scales[:], grouped[:])
+            quantize(codes[:], scales[:], grouped)
             return codes[:], scales[:]
 
-        def knots(number, h, kn, window, width, name):
-            acc = bank(number, [P, width], name)
-            mx_pass(acc[:], h, kn)
-            nc.scalar.copy(window[:, :width], acc[:])
+        def knots(number, h, kn, window, width):
+            acc = banks[number][:, :width]
+            mx_pass(acc, h, kn)
+            nc.scalar.copy(window[:, :width], acc)
 
         kn1_codes = tile("kn1_codes", G, U32)
         kn1_scales = tile("kn1_scales", G, U8)
@@ -165,102 +168,125 @@ def tile_picked_ynhits_val_p_kernel(
         for c0 in range(0, G, P):
             cols = slice(c0, c0 + P)
             quantize(kn1_codes[:, cols], kn1_scales[:, cols], kn1_grouped[:, PACK * c0 : PACK * (c0 + P)])
-        hq = [None] * TILES
-        hq[0] = hidden(0, 0)
-        gather_words(2, TILES, on="h_grouped0")
-        hq[1] = hidden(1, 1)
-        knots(2, hq[0], kn1_q, y1[0], G, "y1_acc0")
-        a1 = tile("a1", R, F32, on="h_grouped1")
-        nc.vector.tensor_scalar(a1[:], f1[:], -1.0, 1.0, ALU.mult, ALU.add)
-        knots(3, hq[1], kn1_q, y1[1], G, "y1_acc1")
-        hq[2] = hidden(2, 2)
-
         kn2_codes = tile("kn2_codes", W, U32)
         kn2_scales = tile("kn2_scales", W, U8)
         kn2_q = (kn2_codes[:], kn2_scales[:])
-        kn2_grouped = tile("kn2_grouped", PACK * W, BF16)
-        for c0 in range(0, W, P):
-            raw = kn2_raw[c0 // G][:, :, c0 % G : c0 % G + P]
-            interleave(nc.scalar.copy, kn2_grouped[:, PACK * c0 : PACK * (c0 + P)], raw)
-        quantize(kn2_codes[:], kn2_scales[:], kn2_grouped[:])
-        knots(0, hq[2], kn1_q, y1[2], G, "y1_acc2")
-        hq[3] = hidden(3, 3)
-        a2 = tile("a2", R, F32)
-        nc.scalar.activation(a2[:], f2[:], ACT.Copy, bias=1.0, scale=-1.0)
-        knots(1, hq[0], kn2_q, y2[0], W, "y2_acc0")
-        knots(2, hq[1], kn2_q, y2[1], W, "y2_acc1")
-        knots(0, hq[2], kn2_q, y2[2], W, "y2_acc2")
-        knots(1, hq[3], kn1_q, y1[3], G, "y1_acc3")
-        knots(2, hq[3], kn2_q, y2[3], W, "y2_acc3")
 
-        def term(name, window, offsets, weight, c0=0, c1=R, on=None):
-            product = tile(name, c1 - c0, F32, on)
-            nc.vector.tensor_tensor(
-                product[:], window[:].indirect(offsets[:, c0 // 16 : c1 // 16]), weight[:, c0:c1], ALU.mult
-            )
-            return product
+        def placed(name, width, dtype, offset):
+            return laid.tile([P, width], dtype, name=name, offset=offset, align_bytes=64)
 
-        def add_turned(turned, part, first, last):
-            chunks = turned.shape[1]
-            for c in range(chunks):
+        def prepare_kn2():
+            held = placed("kn2_grouped", PACK * W, BF16, 2048)
+            grouped = held[:]
+            for u in range(2):
+                interleave(nc.vector.tensor_copy, grouped[:, PACK * u * G : PACK * (u + 1) * G], kn2_raw[u][:])
+            quantize(kn2_codes[:], kn2_scales[:], grouped)
+
+        hq = [None] * TILES
+        windows = {1: y1, 2: y2}
+        lefts = {1: left1_sb, 2: left2_sb}
+        rights = {1: right1_sb, 2: right2_sb}
+        fracs = {1: f1, 2: f2}
+        turned = [banks[number][:].rearrange("p (c n) -> p c n", c=CHUNKS) for number in TURN_BANKS]
+        total = [banks[number] for number in BACK_BANKS]
+        added = [0] * TILES
+        raw = {}
+        part = {}
+
+        def add_turned(t, term):
+            first, last = added[t] == 0, added[t] == 2
+            added[t] += 1
+            for c in range(CHUNKS):
                 nc.tensor.matmul(
-                    turned[:, c, :],
-                    lhsT=part[:, c * P : (c + 1) * P],
+                    turned[t][:, c, :],
+                    lhsT=term[:, c * P : (c + 1) * P],
                     rhs=ident[:],
                     start=first and c == 0,
-                    stop=last and c == chunks - 1,
+                    stop=last and c == CHUNKS - 1,
                     is_transpose=True,
                 )
 
-        def turn_back(turned, number, name):
-            chunks = turned.shape[1]
-            turned_sb = sb.tile([P, chunks, P], F32, name=name + "_turned", align_bytes=64)
-            total = bank(number, [P, chunks * P], name + "_total")
-            for c0 in range(0, chunks, 2):
-                nc.scalar.copy(turned_sb[:, c0 : c0 + 2, :], turned[:, c0 : c0 + 2, :])
-                for c in (c0, c0 + 1):
-                    nc.tensor.transpose(total[:, c * P : (c + 1) * P], turned_sb[:, c, :], ident[:])
-            return total
+        def fresh(name, on):
+            if on is None:
+                held = tile(name, R, F32)
+                return held[:]
+            return on
 
-        last = TILES - 1
-        turned = [bank(4 + t, [P, CHUNKS, P], "turned%d" % t) for t in range(last)]
-        for t in range(last):
-            on = "kn2_raw1" if t == last - 1 else None
-            add_turned(turned[t], term("r1_%d" % t, y1[t], right1_sb, f1, on=on), True, False)
-            add_turned(turned[t], term("l1_%d" % t, y1[t], left1_sb, a1), False, False)
-        for t, back in enumerate((3, 0, 1)):
-            add_turned(turned[t], term("r2_%d" % t, y2[t], right2_sb, f2), False, False)
-            add_turned(turned[t], term("l2_%d" % t, y2[t], left2_sb, a2), False, True)
-            total = turn_back(turned[t], back, "sum%d" % t)
-            result = tile("result%d" % t, R, F32)
-            nc.scalar.copy(result[:], total[:])
-            nc.scalar.dma_start(out[t * P : (t + 1) * P, :], result[:])
+        def fetch_left(rate, t, on=None):
+            raw[rate, t] = fresh("minus_left%d_%d" % (rate, t), on)
+            nc.scalar.activation(raw[rate, t], windows[rate][t][:].indirect(lefts[rate][:]), ACT.Copy, scale=-1.0)
 
-        pieces = [(0, 2), (2, 3), (3, CHUNKS)]
-        turned_last = [bank(number, [P, 1, P], "turned_last%d" % number) for number in (6, 7, 4, 5)]
-        totals = [bank(number, [P, (c1 - c0) * P], "total_last%d" % c0) for number, (c0, c1) in zip((2, 3, 0), pieces)]
+        def left_part(rate, t, turn=True, on=None):
+            part["left", rate, t] = term = fresh("left_part%d_%d" % (rate, t), on)
+            nc.vector.scalar_tensor_tensor(term, fracs[rate][:], -1.0, raw[rate, t], ALU.add, ALU.mult)
+            if turn:
+                add_turned(t, term)
 
-        def add_chunks(part, c0, c1, first, closes):
-            for c in range(c0, c1):
-                add_turned(turned_last[c], part[:, (c - c0) * P : (c - c0 + 1) * P], first, closes)
+        def right_part(rate, t, turn=True, c0=0, c1=R, on=None):
+            part["right", rate, t, c0] = term = fresh("right_part%d_%d_%d" % (rate, t, c0), on)
+            picked = windows[rate][t][:].indirect(rights[rate][:, c0 // 16 : c1 // 16])
+            nc.vector.tensor_tensor(term[:, c0:c1], picked, fracs[rate][:, c0:c1], ALU.mult)
+            if turn:
+                add_turned(t, term)
 
-        def third_term(number):
-            c0, c1 = pieces[number]
-            add_chunks(term("r2_last%d" % c0, y2[last], right2_sb, f2, c0 * P, c1 * P), c0, c1, False, True)
-            for c in range(c0, c1):
-                turned_sb = tile("turned_sb%d" % c, P, F32)
-                nc.scalar.copy(turned_sb[:], turned_last[c][:, 0, :])
-                nc.tensor.transpose(totals[number][:, (c - c0) * P : (c - c0 + 1) * P], turned_sb[:], ident[:])
+        def turn_back(t):
+            turned_sb = sb.tile([P, CHUNKS, P], F32, name="turned_sb%d" % t, align_bytes=64)
+            nc.scalar.copy(turned_sb[:], turned[t])
+            for c in range(CHUNKS):
+                nc.tensor.transpose(total[t][:, c * P : (c + 1) * P], turned_sb[:, c, :], ident[:])
 
-        add_chunks(term("r1_last", y1[last], right1_sb, f1), 0, CHUNKS, True, False)
-        add_chunks(term("l1_last0", y1[last], left1_sb, a1, 0, 2 * P), 0, 2, False, False)
-        third_term(0)
-        add_chunks(term("l1_last2", y1[last], left1_sb, a1, 2 * P, R), 2, CHUNKS, False, False)
-        third_term(1)
-        third_term(2)
-        closing = [term("l2_last%d" % c0, y2[last], left2_sb, a2, c0, c0 + 2 * P) for c0 in (0, 2 * P)]
-        for total, (c0, c1) in zip(totals, pieces):
-            result = tile("result_last%d" % c0, (c1 - c0) * P, F32)
-            fourth = closing[c0 // 2][:, (c0 % 2) * P : (c0 % 2 + c1 - c0) * P]
-            nc.vector.tensor_tensor(result[:], total[:], fourth, ALU.add)
-            nc.sync.dma_start(out[last * P :, c0 * P : c1 * P], result[:])
+        def finish(t, term, c0=0, c1=R):
+            result = tile("result%d_%d" % (t, c0), c1 - c0, F32)
+            nc.vector.tensor_tensor(result[:], total[t][:, c0:c1], term[:, c0:c1], ALU.add)
+            nc.sync.dma_start(out[t * P : (t + 1) * P, c0:c1], result[:])
+
+        term_a, term_b, term_c = (placed("term%d" % at, R, F32, at) for at in (64, 2624, 4672))
+        early = placed("h_grouped1", PACK * P, BF16, 2048)
+        hq[0] = hidden(0, 0)
+        gather_words(2, TILES, on="h_grouped0")
+        hq[1] = hidden(1, 1, early[:])
+        knots(4, hq[0], kn1_q, y1[0], G)
+        knots(5, hq[1], kn1_q, y1[1], G)
+        prepare_kn2()
+        hq[2] = hidden(2, 2, codes=tile("h_codes2", P, U32, on="kn2_raw1"))
+        hq[3] = hidden(3, 3, codes=placed("h_codes3", P, U32, 2112))
+        fetch_left(1, 0)
+        knots(6, hq[2], kn1_q, y1[2], G)
+        knots(0, hq[0], kn2_q, y2[0], W)
+        knots(7, hq[3], kn1_q, y1[3], G)
+        right_part(1, 0, on=term_a[:])
+        fetch_left(1, 1)
+        knots(1, hq[1], kn2_q, y2[1], W)
+        right_part(1, 1, on=term_b[:])
+        left_part(1, 0, on=term_c[:])
+        fetch_left(2, 0)
+        knots(2, hq[2], kn2_q, y2[2], W)
+        knots(3, hq[3], kn2_q, y2[3], W)
+        right_part(1, 2)
+        left_part(1, 1)
+        fetch_left(1, 2)
+        right_part(2, 0)
+        left_part(2, 0, turn=False)
+        fetch_left(2, 1)
+        right_part(2, 1)
+        left_part(1, 2)
+        turn_back(0)
+        fetch_left(1, 3, on=part["right", 2, 0, 0])
+        right_part(2, 2)
+        left_part(2, 1, turn=False)
+        turn_back(1)
+        fetch_left(2, 3, on=part["right", 2, 1, 0])
+        right_part(1, 3)
+        finish(0, part["left", 2, 0])
+        left_part(1, 3)
+        turn_back(2)
+        fetch_left(2, 2, on=part["right", 2, 2, 0])
+        left_part(2, 3)
+        turn_back(3)
+        finish(1, part["left", 2, 1])
+        right_part(2, 3, turn=False, c1=2 * P, on=raw[1, 3])
+        left_part(2, 2, turn=False, on=part["left", 2, 1])
+        finish(2, part["left", 2, 2])
+        right_part(2, 3, turn=False, c0=2 * P, on=raw[2, 2])
+        finish(3, part["right", 2, 3, 0], 0, 2 * P)
+        finish(3, part["right", 2, 3, 2 * P], 2 * P, R)

@@ -22,6 +22,7 @@ TILES = S // P
 CHUNKS = R // P
 WINDOW = R + 16
 TURN_BANKS = (4, 5, 6, 7)
+TURNED_TERMS = (3, 3, 3, 3)
 BACK_BANKS = (0, 1, 2, 3)
 
 
@@ -136,23 +137,21 @@ def tile_picked_ynhits_val_p_kernel(
         on_scalar = cast_w1(nc.scalar.copy, 1, 2, PACK)
         quantize_w1(on_vector, 1, 0, 2)
         quantize_w1(on_scalar, 1, 2, PACK)
-        gather_words(1, 2, on="w1_grouped1_2")
+        gather_words(1, TILES, on="w1_grouped1_2")
 
-        def hidden(number, t, grouped=None, codes=None):
+        def hidden(number, t, grouped):
             cols = slice(t * P, (t + 1) * P)
             acc = banks[number][:].rearrange("p (e n) -> p e n", e=PACK)
             for e in range(PACK):
                 ch = slice(e * P, (e + 1) * P)
                 mx_pass(acc[:, e, :], (w1_codes[:, ch], w1_scales[:, ch]), (xg_words[t], xg_scales[:, cols]))
-            if grouped is None:
-                held = tile("h_grouped%d" % t, PACK * P, BF16)
-                grouped = held[:]
             nc.scalar.activation(grouped.rearrange("p (n e) -> p n e", e=PACK), acc.rearrange("p e n -> p n e"), ACT.Relu)
-            if codes is None:
-                codes = tile("h_codes%d" % t, P, U32)
+            return grouped
+
+        def quantize_hidden(t, grouped, codes):
             scales = tile("h_scales%d" % t, P, U8)
-            quantize(codes[:], scales[:], grouped)
-            return codes[:], scales[:]
+            quantize(codes, scales[:], grouped)
+            return codes, scales[:]
 
         def knots(number, h, kn, window, width):
             acc = banks[number][:, :width]
@@ -163,11 +162,8 @@ def tile_picked_ynhits_val_p_kernel(
         kn1_scales = tile("kn1_scales", G, U8)
         kn1_q = (kn1_codes[:], kn1_scales[:])
         kn1_grouped = tile("kn1_grouped", PACK * G, BF16)
-        for c0 in range(0, G, P):
-            interleave(nc.vector.tensor_copy, kn1_grouped[:, PACK * c0 : PACK * (c0 + P)], kn1_raw[:, :, c0 : c0 + P])
-        for c0 in range(0, G, P):
-            cols = slice(c0, c0 + P)
-            quantize(kn1_codes[:, cols], kn1_scales[:, cols], kn1_grouped[:, PACK * c0 : PACK * (c0 + P)])
+        interleave(nc.scalar.copy, kn1_grouped[:], kn1_raw[:])
+        quantize(kn1_codes[:], kn1_scales[:], kn1_grouped[:])
         kn2_codes = tile("kn2_codes", W, U32)
         kn2_scales = tile("kn2_scales", W, U8)
         kn2_q = (kn2_codes[:], kn2_scales[:])
@@ -175,12 +171,14 @@ def tile_picked_ynhits_val_p_kernel(
         def placed(name, width, dtype, offset):
             return laid.tile([P, width], dtype, name=name, offset=offset, align_bytes=64)
 
-        def prepare_kn2():
-            held = placed("kn2_grouped", PACK * W, BF16, 2048)
-            grouped = held[:]
-            for u in range(2):
-                interleave(nc.vector.tensor_copy, grouped[:, PACK * u * G : PACK * (u + 1) * G], kn2_raw[u][:])
-            quantize(kn2_codes[:], kn2_scales[:], grouped)
+        kn2_grouped = placed("kn2_grouped", PACK * W, BF16, 2048)
+
+        def cast_kn2(u):
+            interleave(nc.vector.tensor_copy, kn2_grouped[:, PACK * u * G : PACK * (u + 1) * G], kn2_raw[u][:])
+
+        def quantize_kn2(u):
+            cols = slice(u * G, (u + 1) * G)
+            quantize(kn2_codes[:, cols], kn2_scales[:, cols], kn2_grouped[:, PACK * u * G : PACK * (u + 1) * G])
 
         hq = [None] * TILES
         windows = {1: y1, 2: y2}
@@ -194,7 +192,7 @@ def tile_picked_ynhits_val_p_kernel(
         part = {}
 
         def add_turned(t, term):
-            first, last = added[t] == 0, added[t] == 2
+            first, last = added[t] == 0, added[t] == TURNED_TERMS[t] - 1
             added[t] += 1
             for c in range(CHUNKS):
                 nc.tensor.matmul(
@@ -207,18 +205,23 @@ def tile_picked_ynhits_val_p_kernel(
                 )
 
         def fresh(name, on):
-            if on is None:
-                held = tile(name, R, F32)
+            if on is None or isinstance(on, str):
+                held = tile(name, R, F32, on)
                 return held[:]
             return on
 
-        def fetch_left(rate, t, on=None):
+        def fetch_left(rate, t, on=None, pieces=((0, R),)):
             raw[rate, t] = fresh("minus_left%d_%d" % (rate, t), on)
-            nc.scalar.activation(raw[rate, t], windows[rate][t][:].indirect(lefts[rate][:]), ACT.Copy, scale=-1.0)
+            for c0, c1 in pieces:
+                picked = windows[rate][t][:].indirect(lefts[rate][:, c0 // 16 : c1 // 16])
+                nc.scalar.activation(raw[rate, t][:, c0:c1], picked, ACT.Copy, scale=-1.0)
 
-        def left_part(rate, t, turn=True, on=None):
+        def left_part(rate, t, turn=True, on=None, pieces=((0, R),)):
             part["left", rate, t] = term = fresh("left_part%d_%d" % (rate, t), on)
-            nc.vector.scalar_tensor_tensor(term, fracs[rate][:], -1.0, raw[rate, t], ALU.add, ALU.mult)
+            for c0, c1 in pieces:
+                nc.vector.scalar_tensor_tensor(
+                    term[:, c0:c1], fracs[rate][:, c0:c1], -1.0, raw[rate, t][:, c0:c1], ALU.add, ALU.mult
+                )
             if turn:
                 add_turned(t, term)
 
@@ -229,64 +232,86 @@ def tile_picked_ynhits_val_p_kernel(
             if turn:
                 add_turned(t, term)
 
+        def fetch_right(rate, t, c1, on=None):
+            raw["right", rate, t] = fresh("right_raw%d_%d" % (rate, t), on)
+            picked = windows[rate][t][:].indirect(rights[rate][:, : c1 // 16])
+            nc.scalar.activation(raw["right", rate, t][:, :c1], picked, ACT.Copy)
+
+        def shared_right_part(rate, t, c1):
+            if c1 < R:
+                right_part(rate, t, turn=False, c0=c1)
+                term = part["right", rate, t, c1]
+            else:
+                part["right", rate, t, 0] = term = fresh("right_part%d_%d" % (rate, t), None)
+            nc.vector.tensor_tensor(term[:, :c1], raw["right", rate, t][:, :c1], fracs[rate][:, :c1], ALU.mult)
+            add_turned(t, term)
+
         def turn_back(t):
             turned_sb = sb.tile([P, CHUNKS, P], F32, name="turned_sb%d" % t, align_bytes=64)
             nc.scalar.copy(turned_sb[:], turned[t])
             for c in range(CHUNKS):
                 nc.tensor.transpose(total[t][:, c * P : (c + 1) * P], turned_sb[:, c, :], ident[:])
 
+        def leave(t):
+            result = tile("result%d" % t, R, F32)
+            nc.scalar.copy(result[:], total[t][:])
+            nc.sync.dma_start(out[t * P : (t + 1) * P, :], result[:])
+
         def finish(t, term, c0=0, c1=R):
             result = tile("result%d_%d" % (t, c0), c1 - c0, F32)
             nc.vector.tensor_tensor(result[:], total[t][:, c0:c1], term[:, c0:c1], ALU.add)
             nc.sync.dma_start(out[t * P : (t + 1) * P, c0:c1], result[:])
 
-        term_a, term_b, term_c = (placed("term%d" % at, R, F32, at) for at in (64, 2624, 4672))
-        early = placed("h_grouped1", PACK * P, BF16, 2048)
-        hq[0] = hidden(0, 0)
-        gather_words(2, TILES, on="h_grouped0")
-        hq[1] = hidden(1, 1, early[:])
+        term_a, term_c = (placed("term%d" % at, R, F32, at) for at in (64, 4160))
+        h_all = tile("h_all", TILES * PACK * P, BF16, on="kn1_raw")
+        h_grouped = [hidden(t, t, h_all[:, t * PACK * P : (t + 1) * PACK * P]) for t in range(TILES)]
+        cast_kn2(0)
+        early = tile("h_codes_early", 2 * P, U32, on="kn2_raw0")
+        hq[0] = quantize_hidden(0, h_grouped[0], early[:, :P])
+        quantize_kn2(0)
+        hq[1] = quantize_hidden(1, h_grouped[1], early[:, P:])
+        cast_kn2(1)
+        later = tile("h_codes_later", 2 * P, U32, on="kn2_raw1")
+        hq[2] = quantize_hidden(2, h_grouped[2], later[:, :P])
+        quantize_kn2(1)
+        hq[3] = quantize_hidden(3, h_grouped[3], later[:, P:])
         knots(4, hq[0], kn1_q, y1[0], G)
         knots(5, hq[1], kn1_q, y1[1], G)
-        prepare_kn2()
-        hq[2] = hidden(2, 2, codes=tile("h_codes2", P, U32, on="kn2_raw1"))
-        hq[3] = hidden(3, 3, codes=placed("h_codes3", P, U32, 2112))
         fetch_left(1, 0)
         knots(6, hq[2], kn1_q, y1[2], G)
-        knots(0, hq[0], kn2_q, y2[0], W)
         knots(7, hq[3], kn1_q, y1[3], G)
-        right_part(1, 0, on=term_a[:])
+        knots(0, hq[0], kn2_q, y2[0], W)
+        right_part(1, 0)
         fetch_left(1, 1)
-        knots(1, hq[1], kn2_q, y2[1], W)
-        right_part(1, 1, on=term_b[:])
+        right_part(1, 1)
         left_part(1, 0, on=term_c[:])
-        fetch_left(2, 0)
+        fetch_left(1, 2)
+        knots(1, hq[1], kn2_q, y2[1], W)
+        right_part(1, 2)
+        left_part(1, 1, on=term_a[:])
+        fetch_right(1, 3, 2 * P)
+        fetch_left(1, 3)
         knots(2, hq[2], kn2_q, y2[2], W)
         knots(3, hq[3], kn2_q, y2[3], W)
-        right_part(1, 2)
-        left_part(1, 1)
-        fetch_left(1, 2)
-        right_part(2, 0)
-        left_part(2, 0, turn=False)
-        fetch_left(2, 1)
-        right_part(2, 1)
         left_part(1, 2)
-        turn_back(0)
-        fetch_left(1, 3, on=part["right", 2, 0, 0])
-        right_part(2, 2)
-        left_part(2, 1, turn=False)
-        turn_back(1)
-        fetch_left(2, 3, on=part["right", 2, 1, 0])
-        right_part(1, 3)
-        finish(0, part["left", 2, 0])
+        fetch_left(2, 0)
+        right_part(2, 0)
+        right_part(2, 1)
+        shared_right_part(1, 3, 2 * P)
         left_part(1, 3)
+        right_part(2, 2)
+        turn_back(0)
+        fetch_left(2, 1, on=part["right", 2, 0, 0])
+        right_part(2, 3)
+        turn_back(1)
         turn_back(2)
         fetch_left(2, 2, on=part["right", 2, 2, 0])
-        left_part(2, 3)
         turn_back(3)
-        finish(1, part["left", 2, 1])
-        right_part(2, 3, turn=False, c1=2 * P, on=raw[1, 3])
-        left_part(2, 2, turn=False, on=part["left", 2, 1])
-        finish(2, part["left", 2, 2])
-        right_part(2, 3, turn=False, c0=2 * P, on=raw[2, 2])
-        finish(3, part["right", 2, 3, 0], 0, 2 * P)
-        finish(3, part["right", 2, 3, 2 * P], 2 * P, R)
+        halves = ((2 * P, R), (0, 2 * P))
+        fetch_left(2, 3, on="y2_2", pieces=halves)
+        for t in range(TILES - 1):
+            left_part(2, t, turn=False)
+            finish(t, part["left", 2, t])
+        left_part(2, 3, turn=False, pieces=halves)
+        for c0, c1 in halves:
+            finish(3, part["left", 2, 3], c0, c1)

@@ -162,7 +162,15 @@ def tile_picked_ynhits_val_p_kernel(
         kn1_scales = tile("kn1_scales", G, U8)
         kn1_q = (kn1_codes[:], kn1_scales[:])
         kn1_grouped = tile("kn1_grouped", PACK * G, BF16)
-        interleave(nc.scalar.copy, kn1_grouped[:], kn1_raw[:])
+        interleave(nc.scalar.copy, kn1_grouped[:, : PACK * P], kn1_raw[:, :, :P])
+        nc.gpsimd.tensor_scalar(
+            kn1_grouped[:, PACK * P :].rearrange("p (c j) -> p c j", j=PACK),
+            kn1_raw[:, :, P:].rearrange("p j c -> p c j"),
+            1.0,
+            0.0,
+            ALU.mult,
+            ALU.add,
+        )
         quantize(kn1_codes[:], kn1_scales[:], kn1_grouped[:])
         kn2_codes = tile("kn2_codes", W, U32)
         kn2_scales = tile("kn2_scales", W, U8)

@@ -123,21 +123,23 @@ def tile_picked_ynhits_val_p_kernel(
                 width = m_half * PACK
                 quantize(w1_codes[:, cols], w1_scales[:, cols], grouped[:, (e - e0) * width : (e - e0 + 1) * width])
 
-        def gather_words(t0, t1, on=None):
-            picked = tile("xg_words%d" % t0, (t1 - t0) * P, U32, on)
-            nc.vector.tensor_copy(picked[:], xw_table[:].bitcast(U32).indirect(offs_sb[:, t0 * P // 16 : t1 * P // 16]))
+        def gather_words(picked, t0, t1):
+            nc.vector.tensor_copy(picked, xw_table[:].bitcast(U32).indirect(offs_sb[:, t0 * P // 16 : t1 * P // 16]))
             for t in range(t0, t1):
                 xg_words[t] = picked[:, (t - t0) * P : (t - t0 + 1) * P]
 
         first_half = cast_w1(nc.scalar.copy, 0, 0, PACK)
         nc.vector.tensor_copy(xg_scales[:], xs_table[:].indirect(offs_sb[:]))
-        gather_words(0, 1)
+        first_words = tile("xg_words0", P, U32)
+        gather_words(first_words[:], 0, 1)
         quantize_w1(first_half, 0, 0, PACK)
         on_vector = cast_w1(nc.vector.tensor_copy, 1, 0, 2)
         on_scalar = cast_w1(nc.scalar.copy, 1, 2, PACK)
         quantize_w1(on_vector, 1, 0, 2)
         quantize_w1(on_scalar, 1, 2, PACK)
-        gather_words(1, TILES, on="w1_grouped1_2")
+        other_words = tile("xg_words1", (TILES - 1) * P, U32, "w1_grouped1_2")
+        gather_words(other_words[:, :P], 1, 2)
+        gather_words(other_words[:, P:], 2, TILES)
 
         def hidden(number, t, grouped):
             cols = slice(t * P, (t + 1) * P)

from contextlib import ExitStack

import concourse.mybir as mybir
from concourse.masks import make_identity

K, T, S, H, R, G, W = 512, 1024, 512, 512, 512, 256, 512
FLOPS = 2 * K * H * S + 2 * H * S * (G + W)

F32 = mybir.dt.float32
BF16 = mybir.dt.bfloat16
I32 = mybir.dt.int32
U32 = mybir.dt.uint32
U16 = mybir.dt.uint16
U8 = mybir.dt.uint8
FP8X4 = mybir.dt.float8_e4m3fn_x4
ACT = mybir.ActivationFunctionType
ALU = mybir.AluOpType

P = 128
PACK = 4
TILES = S // P
CHUNKS = R // P
WINDOW = R + 16
TURN_BANKS = (4, 5, 6, 7)
TURNED_TERMS = (3, 3, 3, 3)
BACK_BANKS = (0, 1, 2, 3)


def tile_picked_ynhits_val_p_kernel(
    tc, x_words, x_scales, w1, kn1, frac1, kn2, frac2, offs, left1, right1, left2, right2, out
):
    nc = tc.nc
    with ExitStack() as ctx:
        lists = ctx.enter_context(tc.tile_pool(name="lists", bufs=1))
        sb = ctx.enter_context(tc.tile_pool(name="sb", bufs=1))
        laid = ctx.enter_context(tc.tile_pool(name="laid", bufs=1))
        psum = ctx.enter_context(tc.psum_pool(name="psum", bufs=1))

        def load_list(name, src):
            held = lists.tile([P, R // 16], U16, name=name)
            nc.sync.dma_start(held[:], src)
            return held

        def load(name, src, shape, dtype):
            held = sb.tile(shape, dtype, name=name, align_bytes=64)
            nc.sync.dma_start(held[:], src)
            return held

        def tile(name, width, dtype, on=None):
            return sb.tile([P, width], dtype, name=name, tag=on or name, align_bytes=64)

        banks = [psum.tile([P, R], F32, name="bank%d" % number) for number in range(8)]

        xs_table = tile("xs_table", T, U8)
        nc.vector.memset(xs_table[:].bitcast(I32), 0)
        ident = tile("ident", P, F32)
        y1 = [tile("y1_%d" % t, WINDOW, F32) for t in range(TILES)]
        y2 = [tile("y2_%d" % t, WINDOW, F32) for t in range(TILES)]
        nc.vector.memset(ident[:], 0.0)
        make_identity(nc, ident[:], nomemset=True)
        for t in range(TILES):
            nc.vector.memset(y1[t][:, G:], 0.0)
            nc.scalar.activation(y2[t][:, W:], y1[0][:, W:], ACT.Relu)

        w1_rows = w1.rearrange("(p j) c -> p j c", j=PACK)
        half = H // 2
        w1_raw = [None, None]
        w1_raw[0] = load("w1_raw0", w1_rows[:, :, :half], [P, PACK, half], F32)
        for q in range(4):
            nc.sync.dma_start(
                xs_table[:].bitcast(I32)[32 * q : 32 * q + 4, :], x_scales[0].bitcast(I32)[4 * q : 4 * q + 4, :]
            )
        offs_sb = load_list("offs_sb", offs)
        xw_table = load("xw_table", x_words[0].rearrange("p n j -> p (n j)").bitcast(I32), [P, T], I32)
        w1_raw[1] = load("w1_raw1", w1_rows[:, :, half:], [P, PACK, half], F32)
        kn1_raw = load("kn1_raw", kn1.rearrange("(p j) c -> p j c", j=PACK), [P, PACK, G], F32)
        left1_sb = load_list("left1_sb", left1)
        kn2_rows = kn2.rearrange("(p j) c -> p j c", j=PACK)
        kn2_raw = [load("kn2_raw%d" % u, kn2_rows[:, :, u * G : (u + 1) * G], [P, PACK, G], F32) for u in range(2)]
        right1_sb = load_list("right1_sb", right1)
        f1 = load("f1", frac1, [P, R], F32)
        left2_sb = load_list("left2_sb", left2)
        right2_sb = load_list("right2_sb", right2)
        f2 = load("f2", frac2, [P, R], F32)

        def quantize(codes, scales, grouped):
            nc.vector.quantize_mx(out=codes.bitcast(FP8X4), scales=scales, in_=grouped)

        def interleave(copy, grouped, raw):
            copy(
                grouped.rearrange("p (c i j) -> p c j i", i=4, j=PACK),
                raw.rearrange("p j (c i) -> p c j i", i=4),
            )

        def mx_pass(acc, lhs, rhs):
            nc.tensor.matmul_mx(
                out=acc,
                lhsT=lhs[0].bitcast(FP8X4),
                lhsT_scale=lhs[1],
                rhs=rhs[0].bitcast(FP8X4),
                rhs_scale=rhs[1],
                start=True,
                stop=True,
            )

        w1_codes = sb.tile([P, H], U32, name="w1_codes", tag="xs_table", align_bytes=64)
        w1_scales = tile("w1_scales", H, U8)
        xg_words = [None] * TILES
        xg_scales = tile("xg_scales", S, U8)
        m_half = P // 2

        def cast_w1(copy, u, e0, e1):
            grouped = tile("w1_grouped%d_%d" % (u, e0), (e1 - e0) * m_half * PACK, BF16)
            copy(
                grouped[:].rearrange("p (e m j) -> p m j e", m=m_half, j=PACK),
                w1_raw[u][:].rearrange("p j (m e) -> p m j e", e=PACK)[:, :, :, e0:e1],
            )
            return grouped

        def quantize_w1(grouped, u, e0, e1):
            for e in range(e0, e1):
                cols = slice(e * P + u * m_half, e * P + (u + 1) * m_half)
                width = m_half * PACK
                quantize(w1_codes[:, cols], w1_scales[:, cols], grouped[:, (e - e0) * width : (e - e0 + 1) * width])

        def gather_words(picked, t0, t1):
            nc.vector.tensor_copy(picked, xw_table[:].bitcast(U32).indirect(offs_sb[:, t0 * P // 16 : t1 * P // 16]))
            for t in range(t0, t1):
                xg_words[t] = picked[:, (t - t0) * P : (t - t0 + 1) * P]

        first_half = cast_w1(nc.scalar.copy, 0, 0, PACK)
        nc.vector.tensor_copy(xg_scales[:], xs_table[:].indirect(offs_sb[:]))
        first_words = tile("xg_words0", P, U32)
        gather_words(first_words[:], 0, 1)
        quantize_w1(first_half, 0, 0, PACK)
        on_vector = cast_w1(nc.vector.tensor_copy, 1, 0, 2)
        on_scalar = cast_w1(nc.scalar.copy, 1, 2, PACK)
        quantize_w1(on_vector, 1, 0, 2)
        quantize_w1(on_scalar, 1, 2, PACK)
        other_words = tile("xg_words1", (TILES - 1) * P, U32, "w1_grouped1_2")
        gather_words(other_words[:, :P], 1, 2)
        gather_words(other_words[:, P:], 2, TILES)

        def hidden(number, t, grouped):
            cols = slice(t * P, (t + 1) * P)
            acc = banks[number][:].rearrange("p (e n) -> p e n", e=PACK)
            for e in range(PACK):
                ch = slice(e * P, (e + 1) * P)
                mx_pass(acc[:, e, :], (w1_codes[:, ch], w1_scales[:, ch]), (xg_words[t], xg_scales[:, cols]))
            nc.scalar.activation(grouped.rearrange("p (n e) -> p n e", e=PACK), acc.rearrange("p e n -> p n e"), ACT.Relu)
            return grouped

        def quantize_hidden(t, grouped, codes):
            scales = tile("h_scales%d" % t, P, U8)
            quantize(codes, scales[:], grouped)
            return codes, scales[:]

        def knots(number, h, kn, window, width):
            acc = banks[number][:, :width]
            mx_pass(acc, h, kn)
            nc.scalar.copy(window[:, :width], acc)

        kn1_codes = tile("kn1_codes", G, U32)
        kn1_scales = tile("kn1_scales", G, U8)
        kn1_q = (kn1_codes[:], kn1_scales[:])
        kn1_grouped = tile("kn1_grouped", PACK * G, BF16)
        interleave(nc.scalar.copy, kn1_grouped[:, : PACK * P], kn1_raw[:, :, :P])
        nc.gpsimd.tensor_scalar(
            kn1_grouped[:, PACK * P :].rearrange("p (c j) -> p c j", j=PACK),
            kn1_raw[:, :, P:].rearrange("p j c -> p c j"),
            1.0,
            0.0,
            ALU.mult,
            ALU.add,
        )
        quantize(kn1_codes[:], kn1_scales[:], kn1_grouped[:])
        kn2_codes = tile("kn2_codes", W, U32)
        kn2_scales = tile("kn2_scales", W, U8)
        kn2_q = (kn2_codes[:], kn2_scales[:])

        def placed(name, width, dtype, offset):
            return laid.tile([P, width], dtype, name=name, offset=offset, align_bytes=64)

        kn2_grouped = placed("kn2_grouped", PACK * W, BF16, 2048)

        def cast_kn2(u):
            interleave(nc.vector.tensor_copy, kn2_grouped[:, PACK * u * G : PACK * (u + 1) * G], kn2_raw[u][:])

        def quantize_kn2(u):
            cols = slice(u * G, (u + 1) * G)
            quantize(kn2_codes[:, cols], kn2_scales[:, cols], kn2_grouped[:, PACK * u * G : PACK * (u + 1) * G])

        hq = [None] * TILES
        windows = {1: y1, 2: y2}
        lefts = {1: left1_sb, 2: left2_sb}
        rights = {1: right1_sb, 2: right2_sb}
        fracs = {1: f1, 2: f2}
        turned = [banks[number][:].rearrange("p (c n) -> p c n", c=CHUNKS) for number in TURN_BANKS]
        total = [banks[number] for number in BACK_BANKS]
        added = [0] * TILES
        raw = {}
        part = {}

        def add_turned(t, term):
            first, last = added[t] == 0, added[t] == TURNED_TERMS[t] - 1
            added[t] += 1
            for c in range(CHUNKS):
                nc.tensor.matmul(
                    turned[t][:, c, :],
                    lhsT=term[:, c * P : (c + 1) * P],
                    rhs=ident[:],
                    start=first and c == 0,
                    stop=last and c == CHUNKS - 1,
                    is_transpose=True,
                )

        def fresh(name, on):
            if on is None or isinstance(on, str):
                held = tile(name, R, F32, on)
                return held[:]
            return on

        def fetch_left(rate, t, on=None, pieces=((0, R),)):
            raw[rate, t] = fresh("minus_left%d_%d" % (rate, t), on)
            for c0, c1 in pieces:
                picked = windows[rate][t][:].indirect(lefts[rate][:, c0 // 16 : c1 // 16])
                nc.scalar.activation(raw[rate, t][:, c0:c1], picked, ACT.Copy, scale=-1.0)

        def left_part(rate, t, turn=True, on=None, pieces=((0, R),)):
            part["left", rate, t] = term = fresh("left_part%d_%d" % (rate, t), on)
            for c0, c1 in pieces:
                nc.vector.scalar_tensor_tensor(
                    term[:, c0:c1], fracs[rate][:, c0:c1], -1.0, raw[rate, t][:, c0:c1], ALU.add, ALU.mult
                )
            if turn:
                add_turned(t, term)

        def right_part(rate, t, turn=True, c0=0, c1=R, on=None):
            part["right", rate, t, c0] = term = fresh("right_part%d_%d_%d" % (rate, t, c0), on)
            picked = windows[rate][t][:].indirect(rights[rate][:, c0 // 16 : c1 // 16])
            nc.vector.tensor_tensor(term[:, c0:c1], picked, fracs[rate][:, c0:c1], ALU.mult)
            if turn:
                add_turned(t, term)

        def fetch_right(rate, t, c1, on=None):
            raw["right", rate, t] = fresh("right_raw%d_%d" % (rate, t), on)
            picked = windows[rate][t][:].indirect(rights[rate][:, : c1 // 16])
            nc.scalar.activation(raw["right", rate, t][:, :c1], picked, ACT.Copy)

        def shared_right_part(rate, t, c1):
            if c1 < R:
                right_part(rate, t, turn=False, c0=c1)
                term = part["right", rate, t, c1]
            else:
                part["right", rate, t, 0] = term = fresh("right_part%d_%d" % (rate, t), None)
            nc.vector.tensor_tensor(term[:, :c1], raw["right", rate, t][:, :c1], fracs[rate][:, :c1], ALU.mult)
            add_turned(t, term)

        def turn_back(t):
            turned_sb = sb.tile([P, CHUNKS, P], F32, name="turned_sb%d" % t, align_bytes=64)
            nc.scalar.copy(turned_sb[:], turned[t])
            for c in range(CHUNKS):
                nc.tensor.transpose(total[t][:, c * P : (c + 1) * P], turned_sb[:, c, :], ident[:])

        def leave(t):
            result = tile("result%d" % t, R, F32)
            nc.scalar.copy(result[:], total[t][:])
            nc.sync.dma_start(out[t * P : (t + 1) * P, :], result[:])

        def finish(t, term, c0=0, c1=R):
            result = tile("result%d_%d" % (t, c0), c1 - c0, F32)
            nc.vector.tensor_tensor(result[:], total[t][:, c0:c1], term[:, c0:c1], ALU.add)
            nc.sync.dma_start(out[t * P : (t + 1) * P, c0:c1], result[:])

        term_a, term_c = (placed("term%d" % at, R, F32, at) for at in (64, 4160))
        h_all = tile("h_all", TILES * PACK * P, BF16, on="kn1_raw")
        h_grouped = [hidden(t, t, h_all[:, t * PACK * P : (t + 1) * PACK * P]) for t in range(TILES)]
        cast_kn2(0)
        early = tile("h_codes_early", 2 * P, U32, on="kn2_raw0")
        hq[0] = quantize_hidden(0, h_grouped[0], early[:, :P])
        quantize_kn2(0)
        hq[1] = quantize_hidden(1, h_grouped[1], early[:, P:])
        cast_kn2(1)
        later = tile("h_codes_later", 2 * P, U32, on="kn2_raw1")
        hq[2] = quantize_hidden(2, h_grouped[2], later[:, :P])
        quantize_kn2(1)
        hq[3] = quantize_hidden(3, h_grouped[3], later[:, P:])
        knots(4, hq[0], kn1_q, y1[0], G)
        knots(5, hq[1], kn1_q, y1[1], G)
        fetch_left(1, 0)
        knots(6, hq[2], kn1_q, y1[2], G)
        knots(7, hq[3], kn1_q, y1[3], G)
        knots(0, hq[0], kn2_q, y2[0], W)
        right_part(1, 0)
        fetch_left(1, 1)
        right_part(1, 1)
        left_part(1, 0, on=term_c[:])
        fetch_left(1, 2)
        knots(1, hq[1], kn2_q, y2[1], W)
        right_part(1, 2)
        left_part(1, 1, on=term_a[:])
        fetch_right(1, 3, 2 * P)
        fetch_left(1, 3)
        knots(2, hq[2], kn2_q, y2[2], W)
        knots(3, hq[3], kn2_q, y2[3], W)
        left_part(1, 2)
        fetch_left(2, 0)
        right_part(2, 0)
        right_part(2, 1)
        shared_right_part(1, 3, 2 * P)
        left_part(1, 3)
        right_part(2, 2)
        turn_back(0)
        fetch_left(2, 1, on=part["right", 2, 0, 0])
        right_part(2, 3)
        turn_back(1)
        turn_back(2)
        fetch_left(2, 2, on=part["right", 2, 2, 0])
        turn_back(3)
        halves = ((2 * P, R), (0, 2 * P))
        fetch_left(2, 3, on="y2_2", pieces=halves)
        for t in range(TILES - 1):
            left_part(2, t, turn=False)
            finish(t, part["left", 2, t])
        left_part(2, 3, turn=False, pieces=halves)
        for c0, c1 in halves:
            finish(3, part["left", 2, 3], c0, c1)
